import numpy as np, ml_dtypes
CORES = [40,64,80,88,96,104,120,144]
N = 8
BF = ml_dtypes.bfloat16
L, S, ST, GENS, K = 128, 9, 4, 2, 32
GW, XW = S * L, 16 * L
def parts(rng):
    g = rng.integers(0, XW, (N, 8, 16, GW)); h = rng.integers(0, GW, (N, 8, 16, GW)); x = rng.integers(0, 256, (N, 8, 16, XW))
    return g, h, x, rng.integers(0, 256, (N, 8, 16, L)), rng.integers(800, 1151, (N, 8))
def pack(g, h, x, a, t):
    return {"gn": np.ascontiguousarray(g.reshape(N, 128, GW)).astype(np.int32), "nb": np.ascontiguousarray(h.reshape(N, 128, GW)).astype(np.int32),
            "x": x.reshape(N, 128, XW).astype(np.float32).astype(BF), "th": np.repeat(t, 16, axis=1).reshape(N, 128, 1).astype(np.int32), "a0": a.reshape(N, 128, L).astype(np.float32).astype(BF)}
def setup_inputs(rng):
    return pack(*parts(rng))
def uneven(rng, n):
    v = np.floor(256 * rng.random((N, 8, 16, n)) * np.exp2(-rng.integers(0, 8, (N, 8, 1, n)).astype(np.float64))).astype(np.int64)
    return np.where(rng.random((N, 8, 1, n)) < 0.5, 255 - v, v)
def setup_inputs_spread(rng):
    g = (XW * rng.random((N, 8, 16, GW)) ** 3).astype(np.int64); h = (GW * rng.random((N, 8, 16, GW)) ** 2).astype(np.int64)
    g[:, 1::2] = XW - 1 - g[:, 1::2]; h[:, :, ::2] = GW - 1 - h[:, :, ::2]
    t = np.argsort(rng.random((N, 8)), axis=1) * 510 + rng.integers(0, 510, (N, 8))
    return pack(g, h, uneven(rng, XW), uneven(rng, L), t)
def twoends(rng, n):
    return np.where(rng.random((N, 8, 1, n)) < 0.7, 255 * rng.integers(0, 2, (N, 8, 1, n)), 255 * rng.integers(0, 2, (N, 8, 16, n)))
def setup_inputs_ends(rng):
    g, h, x, a, t = parts(rng)
    g = np.where(rng.random(g.shape) < 0.8, (XW - 1) * rng.integers(0, 2, g.shape), g); h = np.where(rng.random(h.shape) < 0.8, (GW - 1) * rng.integers(0, 2, h.shape), h)
    x = twoends(rng, XW); a = twoends(rng, L); x[..., 0] = 0; x[..., XW - 1] = 255
    for q in range(N): t[q, :7] = rng.permutation(np.array([0, 0, 4080, 4080, 4080, 2294, 2294]))
    t[:, 7] = 0
    for i in (0, 1, L - 2, L - 1):
        g[:, 7, 0, S * i] = XW - 1; h[:, 7, :, S * i] = GW - 1; a[:, 7, :, i] = 0
    g[:, 7, :15, GW - 1] = XW - 1; g[:, 7, 15, GW - 1] = 0
    return pack(g, h, x, a, t)
def setup_inputs_corners(rng):
    g, h, x, a, t = parts(rng); o = rng.permutation(8); t[:, o[0]] = 0; t[:, o[1]] = 4080
    for q in range(N):
        w = rng.permutation(o[2:])
        h[q, w[0]] = np.arange(GW); h[q, w[1]] = (GW - 1) * rng.integers(0, 2, (16, GW)); h[q, w[2]] = np.roll(np.arange(GW), -1)
        g[q, w[3]] = (XW - 1) * rng.integers(0, 2, (16, GW))
        b = w[4]; t[q, b] = 0; x[q, b, :, XW - 1] = 255; g[q, b, 15] = XW - 1
        i = rng.permutation(L)[:L // 2]; a[q, b][:, i] = x[q, b][:, g[q, b, 0, S * i]]
        x[q, w[5]] = 255 * rng.integers(0, 2, (16, XW))
    return pack(g, h, x, a, t)
def setup_inputs_ties(rng):
    g, h, x, a, t = parts(rng)
    x = 8 * rng.integers(0, 32, (N, 8, 1, XW)) + ((np.arange(16)[:, None] == rng.integers(0, 16, (N, 8, 1, XW))) & (rng.random((N, 8, 1, XW)) < 0.5))
    a = 8 * rng.integers(0, 32, (N, 8, 1, L)) + np.zeros((16, 1), np.int64)
    h[:, ::2] = h[:, ::2, :1]
    return pack(g, h, x, a, 16 * (8 * rng.integers(0, 6, (N, 8)) + 1))
def setup_inputs_counts(rng):
    g, h, x, a, t = parts(rng); q = rng.permutation(N); o = rng.permutation(8); w = int(o[0])
    t[q[0]] = 0; t[q[1]] = 4080; t[q[2]] = 4080; t[q[2], o[1:4]] = 0; t[q[3]] = 0
    if N > 4: t[q[4]] = 1170
    if N > 5: t[q[5], o[1:5]] = 0
    t[:, w] = 0; t[q[1], w] = 4080
    u = np.floor(rng.integers(2, 7, (N, 1, XW)) * rng.random((N, 16, XW))).astype(np.int64); u[:, 0] = 0
    x[:, w] = u; x[q[1], w] = 255 - u[q[1]]; x[q[1], w, 0] = 254
    a[:, w] = 255; a[:, w, 0] = 254
    for r, n in ((q[2], 64), (q[3], 8 * int(rng.integers(3, 5)) + int(rng.choice(np.array([2, 3, 5, 6]))))):
        i = rng.permutation(L)[:n]; a[r, w, 0, i] = 255; h[r, w, 0, S * i] = S * i
    return pack(g, h, x, a, t)
def check_inputs(d):
    bad = []
    for k, lo, hi in (("gn", 0, XW - 1), ("nb", 0, GW - 1), ("x", 0, 255), ("th", 0, 4080), ("a0", 0, 255)):
        v = np.asarray(d[k]).astype(np.float64)
        if not (np.min(v) >= lo and np.max(v) <= hi): bad.append("range of " + k)
        elif np.any(v != np.floor(v)): bad.append("whole numbers of " + k)
    v = np.asarray(d["th"]).reshape(-1, 16)
    if np.any(v != v[:, :1]): bad.append("equal rows of th in a group")
    return bad
def reference(gn, nb, x, th, a0):
    G = gn.astype(np.int64).reshape(N, 8, 16, GW); H = nb.astype(np.int64).reshape(N, 8, 16, GW); X = x.astype(np.float32).astype(np.int64).reshape(N, 8, 16, XW)
    lim = th.astype(np.int64).reshape(N, 8, 16)[:, :, :1]; a = a0.astype(np.float32).astype(np.int64).reshape(N, 8, 16, L)
    A = np.zeros(N, np.int64); lane = np.arange(L); kk = np.arange(16)[None, :, None]
    for gen in range(GENS):
        h = np.zeros((N, 8, L), np.int64) + S * lane; p = np.zeros((N, 8, L), np.int64); err = np.zeros((N, 8, L), np.int64)
        dau = G[..., ::S].copy()
        for t in range(ST):
            now = np.zeros(N, np.int64)
            for r in range(N):
                q = (r + t) % N; hr = h[r][:, None, :]; pr = p[r]
                n = np.take_along_axis(np.take_along_axis(G[q], hr, 2), pr[:, None, :], 1)[:, 0]
                T = np.abs(np.take_along_axis(X[q], n[:, None, :], 2) - a[r])
                ho = np.take_along_axis(H[q], hr, 2)
                at = ((pr[:, None, :] + kk) & 15) * GW + ho
                e = np.take_along_axis(G[q].reshape(8, 16 * GW), at.reshape(8, 16 * L), 1)
                v = np.take_along_axis(X[q], e[:, None, :], 2).reshape(8, 16, 16, L)
                D = np.add.reduce(np.abs(v + T[:, :, None, :] - 255), axis=1)
                ok = D <= (lim[q] + (A[q] & 63))[:, :, None]
                found = np.any(ok, axis=1); m = np.argmax(ok, axis=1)
                em = np.take_along_axis(e.reshape(8, 16, L), m[:, None, :], 1)[:, 0]; hm = np.take_along_axis(ho, m[:, None, :], 1)[:, 0]
                an = np.where(found[:, None, :], np.take_along_axis(X[q], em[:, None, :], 2), T)
                dau[r, :, t] = np.where(found, em, n); h[r] = np.where(found, hm, h[r]); p[r] = (pr + 1 + np.where(found, m, 0)) & 15
                err[r] = err[r] + np.where(found, 0, 1); now[q] = np.sum(np.where(found, 0, 1)); a[r] = an
                np.put_along_axis(X[q], (16 * lane + p[r])[:, None, :], an, 2)
            A = now
        order = np.argsort(err * L + lane, axis=2)
        best = np.take_along_axis(dau, order[:, :, None, :K], 3)
        come = np.where((np.arange(K) & 1) == 1, np.roll(best, 1, axis=0), best)
        worst = order[:, :, ::-1][:, :, :K]
        np.put_along_axis(G, (S * worst)[:, :, None, :], come, 3)
    return {"yg": G[..., ::S].reshape(N, 128, L).astype(np.float32), "ya": a.reshape(N, 128, L).astype(np.float32), "ys": np.add.reduce(X.reshape(N, 8, 16, L, 16), axis=4).reshape(N, 128, L).astype(np.float32)}

@@ -1,0 +1,513 @@
+import numpy as np
+from concourse.bass import DstId, RemoteDMATransfer
+from concourse.mybir import dt, AluOpType, AxisListType, ActivationFunctionType
+
+OP = AluOpType
+AF = ActivationFunctionType
+GENS, ST, N = 2, 4, 8
+NPOOL = 104
+
+F32, F16, BF, I32, U16 = "float32", "float16", "bfloat16", "int32", "uint16"
+SB = {
+    "GW": (1184, I32), "NBW": (1152, I32), "XT": (2176, BF), "A0": (128, BF), "TH": (1, I32),
+    "PI": (1, I32), "PS": (1, I32), "PL": (1, I32), "PSF": (1, F32), "PLF": (1, F32), "PL1": (1, F32), "F4": (1, F32), "ROWM": (1, F32),
+    "MI": (128, I32), "MS": (128, I32), "ML": (128, I32), "ML1": (128, F16), "BLK": (128, F16), "Z": (128, F16),
+    "CRF": (2048, F16), "CRB": (2048, BF), "IDB": (128, BF), "F2": (128, F16), "FIRST": (128, F16), "TRI": (128, F32),
+    "ALL": (128, F32), "ZER": (128, BF), "DI": (64, I32), "DI2": (64, I32), "DELT": (64, BF), "C16": (8, I32), "ILF": (8, F32),
+    "HU0": (16, U16), "NINE": (8, F32), "KC": (8, F32), "B16": (8, I32),
+    "HU": (4 * 8, U16), "NBG": (4 * 64, F32), "OFFE": (4 * 64, U16), "D2": (4 * 128, BF), "MASK": (4 * 1024, BF), "GHM": (4 * 64, F16),
+    "FBT": (4 * 8, F32), "U1": (4 * 4, F32),
+    "NL": (2 * 4, U16), "DD": (2 * 64, BF), "T2": (2 * 128, BF), "TEXP": (2 * 1024, BF), "GG": (2 * 1024, F16), "EL": (2 * 64, U16),
+    "UU": (2 * 1024, F32), "AB": (2 * 1024, BF), "OKT": (2 * 64, F16), "PACK": (2 * 320, F16), "NF": (2 * 8, F32), "TMP": (2 * 8, F32),
+    "IDXF": (2 * 4, F32), "IDX": (2 * 4, U16), "NFB": (2 * 64, F32), "GHF": (2 * 64, F16),
+    "UI": (8, I32), "UI2": (8, I32), "UI3": (8, I32), "POS": (8, U16), "RF": (2, F32), "AI": (1, I32), "AI2": (1, I32), "LIM": (9, F32),
+    "DZ": (128, F16), "IND": (128, F16), "NRED": (1, F32), "PRE": (128, F32), "PPK": (128, F16), "POSL": (8, U16), "SD": (128, F32),
+    "GEC": (8, F32), "DQ": (8, F32), "MLQ": (8, F32), "IDN": (8, U16), "NEW": (128, F32), "YA": (128, F32), "YS": (128, F32),
+    "SA": (16 * 72, F16), "LA": (16 * 72, F16), "SBB": (8 * 256, F16), "LB": (8 * 256, F16), "LE": (4 * 64, F16),
+    "SM": (2 * 24, F16), "LM": (2 * 24, F16), "SO": (2 * 16, F16), "LO": (2 * 16, F16),
+}
+SCRATCH = {}
+for _n in SB:
+    SCRATCH[_n] = ("sbuf", [128, SB[_n][0]], SB[_n][1])
+for _i in range(8):
+    SCRATCH["b%d" % _i] = ("psum", [128, 512], F32)
+
+
+def messages():
+    out = []
+    for g in range(GENS):
+        for t in range(ST):
+            s = g * ST + t
+            if t < ST - 1:
+                for h in range(2):
+                    out.append(("ra%d%d%d" % (g, t, h), 1, ("SA", (2 * s + h) * 72, (2 * s + h) * 72 + 72),
+                                ("LA", (2 * s + 2 + h) * 72, (2 * s + 2 + h) * 72 + 72), h))
+                out.append(("rb%d%d" % (g, t), 1, ("SBB", s * 256, s * 256 + 256), ("LB", (s + 1) * 256, (s + 1) * 256 + 256), 2))
+            else:
+                for h in range(2):
+                    out.append(("re%d%d" % (g, h), N - 3, ("SA", (2 * s + h) * 72, (2 * s + h) * 72 + 64),
+                                ("LE", (2 * g + h) * 64, (2 * g + h) * 64 + 64), h))
+                out.append(("rm%d" % g, N - 3, ("SM", 24 * g, 24 * g + 24), ("LM", 24 * g, 24 * g + 24), 0))
+                out.append(("ro%d" % g, N - 2, ("SO", 16 * g, 16 * g + 16), ("LO", 16 * g, 16 * g + 16), 1))
+    return out
+
+
+MSG = messages()
+SEMAPHORES = [m[0] for m in MSG] + ["ls"] + ["dm%d" % i for i in range(8)] + ["p%d" % i for i in range(NPOOL)]
+
+
+def route(src, dst, topo, pick):
+    if topo.may_write(src, dst):
+        return [src, dst]
+    c = [x for x in topo.cores_of(src) if x != src and topo.may_write(x, dst)]
+    c.sort(key=lambda x: (topo.die(x) != topo.die(src), x))
+    return [src, c[pick % len(c)], dst]
+
+
+def hop(g, T, topo, a, b, src, land, sem):
+    rid, pid = topo.addr(b, a)
+    g.remote_dma(T[land[0]][:, land[1]:land[2]], T[src[0]][:, src[1]:src[2]], T.sem[sem], T.sem["ls"], pid, rid, topo.mask(a, b))
+    return len(topo.engines(a, b))
+
+
+def relay_program(g, core, T, topo):
+    owner = [c for c in T.cores if c in topo.cores_of(core)]
+    total = 0
+    for c in owner:
+        r = T.rank_of(c)
+        for sem, on, src, land, pick in MSG:
+            way = route(c, T.cores[(r + on) % N], topo, pick)
+            if len(way) == 3 and way[1] == core:
+                g.wait_ge(T.sem[sem], len(topo.engines(c, core)))
+                total += hop(g, T, topo, core, way[2], land, land, sem)
+    if total:
+        g.wait_ge(T.sem["ls"], total)
+
+
+def bits(lo, hi, step):
+    if step == 1:
+        return ((1 << (hi - lo)) - 1) << lo
+    m = 0
+    for i in range(lo, hi, step):
+        m |= 1 << i
+    return m
+
+
+class_cache = {}
+
+
+def new_op(P, q, emit, rd, wr, dur, sem=None, amount=1, sdeps=(), lat=0.0):
+    ops, track, banks = P["ops"], P["track"], P["banks"]
+    k = len(ops)
+    deps = set()
+    for acc, isw in [(a, False) for a in rd] + [(a, True) for a in wr]:
+        name = acc[0]
+        key = (acc[1], acc[2], acc[3] if len(acc) > 3 else 1)
+        if key not in class_cache:
+            class_cache[key] = bits(*key)
+        m = class_cache[key]
+        W, R = track.setdefault(name, ([], []))
+        for mm, o in W:
+            if mm & m and o != k:
+                deps.add(o)
+        if isw:
+            for mm, o in R:
+                if mm & m and o != k:
+                    deps.add(o)
+            W[:] = [(mm & ~m, o) for mm, o in W if mm & ~m] + [(m, k)]
+            R[:] = [(mm & ~m, o) for mm, o in R if mm & ~m]
+        else:
+            R.append((m, k))
+        if name in banks:
+            for o in banks[name]:
+                if o != k and ops[o]["q"] != q:
+                    deps.add(o)
+            banks[name][:] = [o for o in banks[name] if ops[o]["q"] == q]
+            banks[name].append(k)
+    banks_fix = None
+    ops.append({"q": q, "emit": emit, "deps": deps, "sdeps": set(sdeps), "dur": dur, "sem": sem, "amount": amount, "lat": lat})
+    return k
+
+
+def order_ops(ops):
+    n = len(ops)
+    wake = 0.06
+    prio = [0.0] * n
+    succ = [[] for _i in range(n)]
+    for k in range(n):
+        for d in ops[k]["deps"] | ops[k]["sdeps"]:
+            succ[d].append(k)
+    for k in range(n - 1, -1, -1):
+        o = ops[k]
+        prio[k] = o["dur"] + o["lat"] + wake + max([prio[s] for s in succ[k]] or [0.0])
+    left = [len(ops[k]["deps"] | ops[k]["sdeps"]) for k in range(n)]
+    ready = {}
+    free = {}
+    cand = {}
+    for k in range(n):
+        free[ops[k]["q"]] = 0.0
+        cand[ops[k]["q"]] = []
+    for k in range(n):
+        if left[k] == 0:
+            cand[ops[k]["q"]].append(k)
+            ready[k] = 0.0
+    fin = [0.0] * n
+    seq = []
+    while len(seq) < n:
+        best = None
+        for q in cand:
+            if not cand[q]:
+                continue
+            if q == "recv":
+                k = min(cand[q], key=lambda x: ready[x])
+                s = ready[k]
+            else:
+                s = max(free[q], min([ready[x] for x in cand[q]]))
+                k = max([x for x in cand[q] if ready[x] <= s + 1e-9], key=lambda x: (prio[x], -x))
+            if best is None or s < best[0]:
+                best = (s, k, q)
+        s, k, q = best
+        cand[q].remove(k)
+        if q != "recv":
+            free[q] = s + ops[k]["dur"]
+        fin[k] = s + ops[k]["dur"] + ops[k]["lat"]
+        seq.append(k)
+        for c in succ[k]:
+            left[c] -= 1
+            ready[c] = max(ready.get(c, 0.0), fin[k] + wake)
+            if left[c] == 0:
+                cand[ops[c]["q"]].append(c)
+    return seq, max(fin)
+
+
+def emit_ops(g, T, ops, seq):
+    known, clk, waits, waited = {}, {}, {}, set()
+    pos = {k: i for i, k in enumerate(seq)}
+    for k in seq:
+        o = ops[k]
+        if o["q"] == "recv":
+            clk[k] = 0
+            continue
+        kn = known.get(o["q"], 0)
+        w = []
+        for d in sorted(o["deps"], key=lambda x: -pos[x]):
+            if not (kn >> d) & 1:
+                w.append(d)
+                waited.add(d)
+                kn |= (1 << d) | clk[d]
+        known[o["q"]] = kn
+        clk[k] = kn
+        waits[k] = w
+    Q = {"V": g.vector, "P": g.tensor, "S": g.scalar, "Y": g.sync, "G": g}
+    last, count, at = {}, {}, {}
+    pool = ["p%d" % i for i in range(NPOOL)]
+    turn = {}
+    for k in seq:
+        o = ops[k]
+        if o["q"] == "recv":
+            at[k] = (o["sem"], o["amount"])
+            continue
+        q = Q[o["q"]]
+        for d in waits[k]:
+            q.wait_ge(T.sem[at[d][0]], at[d][1])
+        ins = o["emit"]()
+        if k in waited:
+            if o["sem"] is not None:
+                at[k] = (o["sem"], o["amount"])
+                ins.then_inc(T.sem[o["sem"]], o["amount"])
+            else:
+                s = None
+                for c in pool:
+                    if (c not in last) or (clk[k] >> last[c]) & 1:
+                        if s is None or turn.get(c, -1) < turn.get(s, -1):
+                            s = c
+                            if c not in last:
+                                break
+                count[s] = count.get(s, 0) + 1
+                last[s] = k
+                turn[s] = pos[k]
+                at[k] = (s, count[s])
+                ins.then_inc(T.sem[s], 1)
+        elif o["sem"] is not None:
+            at[k] = (o["sem"], o["amount"])
+            ins.then_inc(T.sem[o["sem"]], o["amount"])
+            q.wait_ge(T.sem[o["sem"]], o["amount"])
+
+
+def rank_program(g, core, T, topo):
+    rank = T.rank_of(core)
+    if rank is None:
+        relay_program(g, core, T, topo)
+        return
+    P = {"ops": [], "track": {}, "banks": {"b%d" % i: [] for i in range(8)}}
+    C = 0.00095
+
+    def ap(a):
+        if len(a) > 3:
+            return T[a[0]][:, a[1]:a[2]:a[3]]
+        return T[a[0]][:, a[1]:a[2]]
+
+    def width(a):
+        return len(range(a[1], a[2], a[3] if len(a) > 3 else 1))
+
+    def two(*accs):
+        return all((a[0] in SB and SB[a[0]][1] in (F16, BF, U16)) for a in accs)
+
+    def vdur(n, f):
+        return 0.01 + C * max(64, n * f)
+
+    def cols(*xs):
+        return [x for x in xs if isinstance(x, tuple)]
+
+    def val(x):
+        return ap(x) if isinstance(x, tuple) else x
+
+    def copy(out, in_):
+        new_op(P, "V", lambda: g.vector.tensor_copy(out=ap(out), in_=ap(in_)), [in_], [out], vdur(width(out), 0.5 if two(out, in_) else 1))
+
+    def ts(out, in0, s1, op0, s2=None, op1=None):
+        def e():
+            if op1 is None:
+                return g.vector.tensor_scalar(out=ap(out), in0=ap(in0), scalar1=val(s1), scalar2=None, op0=op0)
+            return g.vector.tensor_scalar(out=ap(out), in0=ap(in0), scalar1=val(s1), scalar2=val(s2), op0=op0, op1=op1)
+        new_op(P, "V", e, [in0] + cols(s1, s2), [out], vdur(width(out), 0.5 if two(out, in0) else 1))
+
+    def tt(out, in0, in1, op):
+        f = 2 if (in0[0] in SB and in1[0] in SB) else 1
+        new_op(P, "V", lambda: g.vector.tensor_tensor(out=ap(out), in0=ap(in0), in1=ap(in1), op=op), [in0, in1], [out], vdur(width(out), f))
+
+    def gather(out, win, off):
+        new_op(P, "V", lambda: g.vector.tensor_copy(out=ap(out), in_=ap(win).indirect(ap(off))), [win, off], [out], 0.05 + 1.6 * C * width(out))
+
+    def gather2(out, win, off, in1, op):
+        new_op(P, "V", lambda: g.vector.tensor_tensor(out=ap(out), in0=ap(win).indirect(ap(off)), in1=ap(in1), op=op), [win, off, in1], [out],
+               0.05 + 1.6 * C * width(out))
+
+    def scatter(win, off, in_):
+        new_op(P, "V", lambda: g.vector.tensor_copy(out=ap(win).indirect(ap(off)), in_=ap(in_)), [off, in_], [win], 0.05 + 3.5 * C * width(in_))
+
+    def fill(out, c):
+        new_op(P, "V", lambda: g.vector.memset(ap(out), c), [], [out], vdur(width(out), 1))
+
+    def act(out, in_, func, accum=None, **kw):
+        def e():
+            if accum is None:
+                return g.scalar.activation(out=ap(out), in_=ap(in_), func=func, **kw)
+            return g.scalar.activation(out=ap(out), in_=ap(in_), func=func, accum_out=ap(accum), **kw)
+        new_op(P, "S", e, [in_], [out] + cols(accum), 0.05 + C * width(out))
+
+    def mms(out, pairs):
+        def e():
+            ins = None
+            for i, (l, r) in enumerate(pairs):
+                ins = g.tensor.matmul(ap(out), ap(l), ap(r), i == 0, i == len(pairs) - 1)
+            return ins
+        f = 4 if SB[pairs[0][0][0]][1] == F32 else 1
+        new_op(P, "P", e, [x for p in pairs for x in p], [out], 0.02 + len(pairs) * C * f * max(64, width(out)))
+
+    def iota(out, pattern, base, cm):
+        new_op(P, "G", lambda: g.iota(ap(out), pattern, base, cm), [], [out], 0.13 + 2 * C * width(out))
+
+    def load(q, out, name, sem):
+        eng = g.sync if q == "Y" else g.scalar
+        new_op(P, q, lambda: eng.dma_start(out=ap(out), in_=T[name][:, :]), [], [out], 0.1, sem=sem, amount=16, lat=3.0)
+
+    def store(name, in_, sem):
+        new_op(P, "Y", lambda: g.sync.dma_start(out=T[name][:, :], in_=ap(in_)), [in_], [], 0.1, sem=sem, amount=16, lat=2.0)
+
+    sent = [0]
+    by = {m[0]: m for m in MSG}
+
+    def send(sem):
+        m = by[sem]
+        way = route(core, T.cores[(rank + m[1]) % N], topo, m[4])
+
+        def e():
+            sent[0] += hop(g, T, topo, core, way[1], m[2], m[3], sem)
+        k = new_op(P, "G", e, [m[2]], [], 1.0)
+        back = T.cores[(rank - m[1]) % N]
+        cnt = len(topo.engines(route(back, core, topo, m[4])[-2], core))
+        new_op(P, "recv", None, [], [m[3]], 0.0, sem=sem, amount=cnt, sdeps=(k,), lat=4.0)
+
+    def sl(name, i, w, lo=0, hi=None, step=1):
+        hi = w if hi is None else hi
+        if step == 1:
+            return (name, i * w + lo, i * w + hi)
+        return (name, i * w + lo, i * w + hi, step)
+
+    def C16F(r): return ("CRF", 128 * r, 128 * r + 128)
+    def C16B(r): return ("CRB", 128 * r, 128 * r + 128)
+    NBWIN, GWIN, XWIN, XALL = ("NBW", 0, 1152), ("GW", 0, 1152), ("XT", 0, 2048), ("XT", 0, 2176)
+    full = lambda n: (n, 0, SB[n][0])
+
+    load("Y", NBWIN, "nb", "dm0")
+    load("S", GWIN, "gn", "dm1")
+    load("Y", full("A0"), "a0", "dm2")
+    load("S", full("TH"), "th", "dm3")
+    load("Y", XWIN, "x", "dm4")
+    iota(full("PI"), [[1, 1]], 0, 1)
+    iota(full("MI"), [[1, 128]], 0, 0)
+    iota(full("C16"), [[16, 8]], 0, 0)
+    iota(full("DI"), [[-1, 64]], 64, 1)
+    ts(full("PS"), full("PI"), 4, OP.arith_shift_right)
+    ts(full("PL"), full("PI"), 15, OP.bitwise_and)
+    copy(full("PSF"), full("PS"))
+    copy(full("PLF"), full("PL"))
+    ts(full("ILF"), full("C16"), full("PLF"), OP.add)
+    fill(full("HU0"), 0)
+    for h in range(2):
+        ts(("HU0", 8 * h, 8 * h + 4), ("ILF", 4 * h, 4 * h + 4), 9.0, OP.mult)
+    ts(full("DI2"), full("DI"), 15, OP.bitwise_and)
+    copy(full("DELT"), full("DI2"))
+    ts(full("MS"), full("MI"), 4, OP.arith_shift_right)
+    ts(full("ML"), full("MI"), 15, OP.bitwise_and)
+    ts(full("ML1"), full("ML"), 1.0, OP.add)
+    ts(full("BLK"), full("MS"), full("PSF"), OP.is_equal)
+    tt(full("Z"), full("ML1"), full("BLK"), OP.mult)
+    for r in range(16):
+        ts(C16F(r), full("Z"), float(r + 1), OP.is_equal)
+    for r in range(16):
+        ts(C16B(r), full("Z"), float(r + 1), OP.is_equal)
+    ts(full("PL1"), full("PLF"), 1.0, OP.add)
+    ts(full("IDB"), full("Z"), full("PL1"), OP.is_equal)
+    ts(full("F2"), full("Z"), full("PL1"), OP.is_gt, 2.0, OP.mult)
+    tt(full("FIRST"), full("F2"), full("IDB"), OP.add)
+    ts(full("TRI"), full("Z"), full("PL1"), OP.is_gt)
+    ts(full("F4"), full("PLF"), -1.0, OP.mult, 4.0, OP.add)
+    ts(full("ROWM"), full("PLF"), 4.0, OP.is_ge)
+    fill(full("ALL"), 0.0625)
+    fill(full("ZER"), 0.0)
+    ts(full("NINE"), full("ILF"), 9.0, OP.mult)
+    ts(full("KC"), full("ILF"), -9.0, OP.mult, 1280.0, OP.add)
+    ts(full("B16"), full("ILF"), 16.0, OP.mult)
+    for s in range(4):
+        h = s & 1
+        ts(sl("FBT", s, 8, 0, 4), ("ILF", 4 * h, 4 * h + 4), 2048.0, OP.add)
+    copy(("LIM", 0, 1), full("TH"))
+
+    for gen in range(GENS):
+        ts(full("DZ"), ("GW", 0, 1152, 9), full("ROWM"), OP.mult)
+        for t in range(ST):
+            n = gen * ST + t
+            end = t == ST - 1
+            for h in range(2):
+                s4 = 2 * (n & 1) + h
+                b = ["b%d" % (4 * h + i) for i in range(4)]
+                la = (2 * n + h) * 72
+                if t == 0:
+                    hl, ul = ("HU0", 8 * h, 8 * h + 4), ("HU0", 8 * h + 4, 8 * h + 8)
+                    ts(sl("FBT", s4, 8, 4, 8), ("ILF", 4 * h, 4 * h + 4), 9.0, OP.mult)
+                    fill(sl("U1", s4, 4), 1.0)
+                    a = ("A0", 64 * h, 64 * h + 64) if gen == 0 else ("LE", 64 * h, 64 * h + 64)
+                else:
+                    hl, ul = sl("HU", s4, 8, 0, 4), sl("HU", s4, 8, 4, 8)
+                    copy(sl("HU", s4, 8), ("LA", la + 64, la + 72))
+                    copy(sl("FBT", s4, 8, 4, 8), ("LA", la + 64, la + 68))
+                    ts(sl("U1", s4, 4), ("LA", la + 68, la + 72), 1.0, OP.add)
+                    a = ("LA", la, la + 64)
+                gather(sl("D2", s4, 128, 0, 128, 2), full("DELT"), ul)
+                gather(sl("NBG", s4, 64), NBWIN, hl)
+                ts(sl("D2", s4, 128, 1, 128, 2), sl("D2", s4, 128, 0, 128, 2), -8.0, OP.add)
+                for k in range(8):
+                    ts(sl("MASK", s4, 1024, k, 1024, 8), sl("D2", s4, 128), float(k), OP.is_equal)
+                gather2(sl("GHM", s4, 64), GWIN, hl, sl("MASK", s4, 1024, 0, 1024, 16), OP.mult)
+                copy(sl("OFFE", s4, 64), sl("NBG", s4, 64))
+                mms((b[0], 0, 4), [(C16F(r), sl("GHM", s4, 64, r, 64, 16)) for r in range(16)])
+                copy(sl("NL", h, 4), (b[0], 0, 4))
+                gather2(sl("DD", h, 64), XWIN, sl("NL", h, 4), a, OP.subtract)
+                for j in range(2):
+                    act(sl("T2", h, 128, j, 128, 2), sl("DD", h, 64), AF.Abs)
+                for k in range(8):
+                    act(sl("TEXP", h, 1024, k, 1024, 8), sl("T2", h, 128), AF.Copy)
+                act(("XT", 2048 + 64 * h, 2112 + 64 * h), sl("DD", h, 64), AF.Abs)
+                gather2(sl("GG", h, 1024), GWIN, sl("OFFE", s4, 64), sl("MASK", s4, 1024), OP.mult)
+                mms((b[1], 0, 64), [(C16F(k), sl("GG", h, 1024, k, 1024, 16)) for k in range(16)])
+                copy(sl("EL", h, 64), (b[1], 0, 64))
+                for q in range(2):
+                    gather2(sl("UU", h, 1024, 512 * q, 512 * q + 512), XWIN, sl("EL", h, 64, 32 * q, 32 * q + 32),
+                            sl("TEXP", h, 1024, 512 * q, 512 * q + 512), OP.add)
+                    act(sl("AB", h, 1024, 512 * q, 512 * q + 512), sl("UU", h, 1024, 512 * q, 512 * q + 512), AF.Abs, bias=-255.0)
+                mms((b[2], 0, 64), [(C16B(k), sl("AB", h, 1024, k, 1024, 16)) for k in range(16)])
+                ts(sl("OKT", h, 64), (b[2], 0, 64), ("LIM", n, n + 1), OP.is_le)
+                mms((b[2], 0, 64), [(full("FIRST"), sl("OKT", h, 64))])
+                sel = sl("PACK", h, 320, 128, 192)
+                ts(sel, (b[2], 0, 64), 1.0, OP.is_equal)
+                ts(sl("PACK", h, 320, 192, 256), (b[2], 0, 64), 1.0, OP.is_equal)
+                ts(sl("PACK", h, 320, 256, 320), (b[2], 0, 64), 1.0, OP.is_equal, full("PLF"), OP.mult)
+                tt(sl("PACK", h, 320, 0, 64), sel, (b[1], 0, 64), OP.mult)
+                tt(sl("PACK", h, 320, 64, 128), sel, sl("NBG", s4, 64), OP.mult)
+                mms((b[0], 0, 20), [(C16F(r), sl("PACK", h, 320, r, 320, 16)) for r in range(16)])
+                ts(sl("NF", h, 8), (b[0], 8, 16), -1.0, OP.mult, 1.0, OP.add)
+                tt(sl("TMP", h, 8), sl("NF", h, 8), sl("FBT", s4, 8), OP.mult)
+                tt(sl("IDXF", h, 4), sl("TMP", h, 8, 0, 4), (b[0], 0, 4), OP.add)
+                copy(sl("IDX", h, 4), sl("IDXF", h, 4))
+                sa = (2 * n + h) * 72
+                if not end:
+                    tt(("SA", sa + 64, sa + 68), sl("TMP", h, 8, 4, 8), (b[0], 4, 8), OP.add)
+                tt(("SA", sa + 68, sa + 72), sl("U1", s4, 4), (b[0], 16, 20), OP.add)
+                gather(("SA", sa, sa + 64), XALL, sl("IDX", h, 4))
+                send("re%d%d" % (gen, h) if end else "ra%d%d%d" % (gen, t, h))
+                mms((b[3], 0, 64), [(full("BLK"), sel)])
+                act(sl("NFB", h, 64), (b[3], 0, 64), AF.Identity, accum=("RF", h, h + 1), scale=-1.0, bias=1.0)
+                fo = ("SBB", 256 * n + 128 + 64 * h, 256 * n + 192 + 64 * h)
+                if t == 0:
+                    copy(fo, (b[3], 0, 64))
+                else:
+                    tt(fo, ("LB", 256 * n + 128 + 64 * h, 256 * n + 192 + 64 * h), (b[3], 0, 64), OP.add)
+                tt(sl("GHF", h, 64), sl("GHM", s4, 64), sl("NFB", h, 64), OP.mult)
+                mms((b[3], 64, 128), [(C16F(t), sl("PACK", h, 320, 0, 64)), (C16F(t), sl("GHF", h, 64))])
+                prev = ("DZ", 64 * h, 64 * h + 64) if t == 0 else ("LB", 256 * n + 64 * h, 256 * n + 64 * h + 64)
+                tt(("SBB", 256 * n + 64 * h, 256 * n + 64 * h + 64), prev, (b[3], 64, 128), OP.add)
+            if not end:
+                send("rb%d%d" % (gen, t))
+            for h in range(2):
+                sa = (2 * n + h) * 72
+                copy(("UI", 4 * h, 4 * h + 4), ("SA", sa + 68, sa + 72))
+            ts(full("UI2"), full("UI"), 15, OP.bitwise_and)
+            tt(full("UI3"), full("UI2"), full("B16"), OP.add)
+            copy(full("POS"), full("UI3"))
+            for h in range(2):
+                sa = (2 * n + h) * 72
+                scatter(XWIN, ("POS", 4 * h, 4 * h + 4), ("SA", sa, sa + 64))
+            if n < GENS * ST - 1:
+                mms(("b3", 128, 129), [(full("ALL"), ("RF", 0, 1)), (full("ALL"), ("RF", 1, 2))])
+                copy(full("AI"), ("b3", 128, 129))
+                ts(full("AI2"), full("AI"), 63, OP.bitwise_and)
+                tt(("LIM", n + 1, n + 2), full("AI2"), full("TH"), OP.add)
+        n = gen * ST + ST - 1
+        ts(full("IND"), ("SBB", 256 * n + 128, 256 * n + 256), full("F4"), OP.is_equal)
+        new_op(P, "V", lambda: g.vector.tensor_reduce(out=ap(full("NRED")), in_=ap(full("IND")), axis=AxisListType.X, op=OP.add),
+               [full("IND")], [full("NRED")], 0.15)
+        mms(("b0", 32, 33), [(full("TRI"), full("NRED"))])
+        new_op(P, "V", lambda: g.vector.tensor_tensor_scan(out=ap(full("PRE")), data0=ap(full("ZER")), data1=ap(full("IND")),
+                                                           initial=ap(("b0", 32, 33)), op0=OP.add, op1=OP.add),
+               [full("IND"), full("ZER"), ("b0", 32, 33)], [full("PRE")], 0.15)
+        tt(full("PPK"), full("PRE"), full("IND"), OP.mult)
+        mms(("b4", 0, 8), [(C16F(r), ("PPK", r, 128, 16)) for r in range(16)])
+        ts(full("POSL"), ("b4", 0, 8), -1.0, OP.add)
+        scatter(full("SD"), full("POSL"), ("SBB", 256 * n, 256 * n + 128))
+        copy(("SM", 24 * gen + 8, 24 * gen + 24), ("SD", 0, 32, 2))
+        copy(("SO", 16 * gen, 16 * gen + 16), ("SD", 1, 32, 2))
+        ts(full("GEC"), ("b4", 0, 8), 97.0, OP.is_ge)
+        tt(full("DQ"), full("KC"), ("b4", 0, 8), OP.subtract)
+        tt(full("MLQ"), full("GEC"), full("DQ"), OP.mult)
+        tt(("SM", 24 * gen, 24 * gen + 8), full("MLQ"), full("NINE"), OP.add)
+        send("rm%d" % gen)
+        send("ro%d" % gen)
+        copy(full("IDN"), ("LM", 24 * gen, 24 * gen + 8))
+        copy(("GW", 1152, 1184, 2), ("LM", 24 * gen + 8, 24 * gen + 24))
+        copy(("GW", 1153, 1184, 2), ("LO", 16 * gen, 16 * gen + 16))
+        gather(full("NEW"), ("GW", 0, 1184), full("IDN"))
+        if gen < GENS - 1:
+            copy(("GW", 0, 1152, 9), full("NEW"))
+    store("yg", full("NEW"), "dm5")
+    for h in range(2):
+        copy(("YA", 64 * h, 64 * h + 64), ("LE", 128 + 64 * h, 192 + 64 * h))
+    store("ya", full("YA"), "dm6")
+    mms(("b7", 0, 128), [(full("IDB"), ("XT", j, 2048, 16)) for j in range(16)])
+    copy(full("YS"), ("b7", 0, 128))
+    store("ys", full("YS"), "dm7")
+
+    seq, total = order_ops(P["ops"])
+    emit_ops(g, T, P["ops"], seq)
+    g.wait_ge(T.sem["ls"], sent[0])

@@ -5,26 +5,37 @@ from concourse.mybir import dt, AluOpType, AxisListType, ActivationFunctionType
 OP = AluOpType
 AF = ActivationFunctionType
 GENS, ST, N = 2, 4, 8
-NPOOL = 104
+BATCH = [(0, 64), (64, 64)]
+NBAT = len(BATCH)
+GCH = 256
+GGQ = "SVSS"
+LOADS = (3.5, 1.5, 1.5, 0.1)
+FARUS = 4.5
+LATE = 3.0
+EXPQ = "VVVVSSSS"
+EVAC = "SVSSV"
+HS = 48
 
 F32, F16, BF, I32, U16 = "float32", "float16", "bfloat16", "int32", "uint16"
 SB = {
-    "GW": (1184, I32), "NBW": (1152, I32), "XT": (2176, BF), "A0": (128, BF), "TH": (1, I32),
-    "PI": (1, I32), "PS": (1, I32), "PL": (1, I32), "PSF": (1, F32), "PLF": (1, F32), "PL1": (1, F32), "F4": (1, F32), "ROWM": (1, F32),
-    "MI": (128, I32), "MS": (128, I32), "ML": (128, I32), "ML1": (128, F16), "BLK": (128, F16), "Z": (128, F16),
-    "CRF": (2048, F16), "CRB": (2048, BF), "IDB": (128, BF), "F2": (128, F16), "FIRST": (128, F16), "TRI": (128, F32),
-    "ALL": (128, F32), "ZER": (128, BF), "DI": (64, I32), "DI2": (64, I32), "DELT": (64, BF), "C16": (8, I32), "ILF": (8, F32),
-    "HU0": (16, U16), "NINE": (8, F32), "KC": (8, F32), "B16": (8, I32),
-    "HU": (4 * 8, U16), "NBG": (4 * 64, F32), "OFFE": (4 * 64, U16), "D2": (4 * 128, BF), "MASK": (4 * 1024, BF), "GHM": (4 * 64, F16),
-    "FBT": (4 * 8, F32), "U1": (4 * 4, F32),
-    "NL": (2 * 4, U16), "DD": (2 * 64, BF), "T2": (2 * 128, BF), "TEXP": (2 * 1024, BF), "GG": (2 * 1024, F16), "EL": (2 * 64, U16),
-    "UU": (2 * 1024, F32), "AB": (2 * 1024, BF), "OKT": (2 * 64, F16), "PACK": (2 * 320, F16), "NF": (2 * 8, F32), "TMP": (2 * 8, F32),
-    "IDXF": (2 * 4, F32), "IDX": (2 * 4, U16), "NFB": (2 * 64, F32), "GHF": (2 * 64, F16),
-    "UI": (8, I32), "UI2": (8, I32), "UI3": (8, I32), "POS": (8, U16), "RF": (2, F32), "AI": (1, I32), "AI2": (1, I32), "LIM": (9, F32),
-    "DZ": (128, F16), "IND": (128, F16), "NRED": (1, F32), "PRE": (128, F32), "PPK": (128, F16), "POSL": (8, U16), "SD": (128, F32),
-    "GEC": (8, F32), "DQ": (8, F32), "MLQ": (8, F32), "IDN": (8, U16), "NEW": (128, F32), "YA": (128, F32), "YS": (128, F32),
-    "SA": (16 * 72, F16), "LA": (16 * 72, F16), "SBB": (8 * 256, F16), "LB": (8 * 256, F16), "LE": (4 * 64, F16),
-    "SM": (2 * 24, F16), "LM": (2 * 24, F16), "SO": (2 * 16, F16), "LO": (2 * 16, F16),
+    "GW": (1152, I32), "NBR": (16 * 1152, I32), "NBF": (1152, F16), "XT": (2064, BF), "A0": (128, BF), "TH": (1, I32),
+    "PI": (1, I32), "PS": (1, I32), "PL": (1, I32), "PSF": (1, F32), "PLF": (1, F32), "PL1": (1, F32), "PN": (1, I32), "PNF": (1, F32),
+    "C1S": (1, F32), "PLM": (1, F32), "ROWM": (1, F32), "MI": (128, I32), "MS": (128, I32), "ML": (128, I32), "ML1": (128, F16),
+    "BLK": (128, F16), "Z": (128, F16), "ZD": (128, F16), "RI": (128, I32), "RJ": (128, I32), "RK": (128, F16), "ZR": (128, F16),
+    "CRF": (2048, F16), "DIAG": (2048, F16), "ROT": (2048, F16), "ID": (128, F16), "ID2": (128, F16), "IDB": (128, BF), "FM": (128, F16), "FH": (128, F16),
+    "NEG3": (128, F16), "IDR": (128, F16), "TRI": (128, F32), "ALL": (128, F32), "ZER": (128, F16), "ONES": (128, F16),
+    "WI": (32, I32), "WJ": (32, I32), "WM": (32, F32), "WT": (2080, BF), "IOTA": (2064, I32), "C16": (8, I32), "ILF": (8, F32),
+    "L0": (16, U16), "KC": (8, F32), "BASE": (4 * 32, F16), "BASE3": (16, F16),
+    "OFF": (3 * 128, U16), "WW": (3 * 128, F16), "M0": (3 * 128, F16), "HT": (3 * 128, F16), "DH": (3 * 128, F16), "GHM": (2 * 128, F16),
+    "DD": (128, BF), "T2": (256, BF), "TEXP": (2048, BF), "GG": (2048, F16), "EL": (128, U16), "UU": (2048, F16), "AB": (2048, F16),
+    "OK": (128, F16), "OKW": (128, F16), "SEL": (128, F16), "PACK": (512, F16), "NF": (128, F16), "NFT": (128, BF), "EN": (16, U16),
+    "RF": (NBAT, F32), "AI": (1, I32), "AI2": (1, I32), "LIM": (9, F32),
+    "HF": (48, F32), "HZ": (48, F32), "HM": (48, F32), "HV": (48, F32), "VL": (48, U16), "E1": (8, F32), "E2": (8, F32), "EU": (8, U16),
+    "CM": (128, F16), "VT": (3 * 128, F16), "GHF": (128, F16), "DT": (128, F16), "IND": (128, F16), "NRED": (1, F32), "PRE": (128, F32),
+    "PPK": (128, F16), "POSL": (8, U16), "SD": (128, F32), "GEC": (8, F32), "DQ": (8, F32), "MLQ": (8, F32), "IDN": (8, U16),
+    "OW": (160, F32), "NEW": (128, F32), "YA": (128, F32), "YS": (128, F32),
+    "H": (GENS * ST * NBAT * HS, U16), "SA": (GENS * ST * 128, BF), "LA": (GENS * ST * 128, BF), "DZ": (GENS * ST * 128, F16),
+    "SM": (GENS * 24, F16), "LM": (GENS * 24, F16), "SO": (GENS * 16, F16), "LO": (GENS * 16, F16),
 }
 SCRATCH = {}
 for _n in SB:
@@ -33,27 +44,35 @@ for _i in range(8):
     SCRATCH["b%d" % _i] = ("psum", [128, 512], F32)
 
 
+def lists_at(n, b, lo, hi):
+    c = BATCH[b][1] // 16
+    at = (n * NBAT + b) * HS
+    return ("H", at + lo * c, at + hi * c)
+
+
 def messages():
-    out = []
+    out = {}
     for g in range(GENS):
         for t in range(ST):
-            s = g * ST + t
+            n = g * ST + t
+            for b, (l0, w) in enumerate(BATCH):
+                if t < ST - 1:
+                    o = 2 * (ST - 1 - t)
+                    out["rl%d%d" % (n, b)] = (1, lists_at(n, b, o, 11), lists_at(n + 1, b, o, 11), b % 2)
+                out["ra%d%d" % (n, b)] = (1 if t < ST - 1 else N - ST + 1, ("SA", 128 * n + l0, 128 * n + l0 + w),
+                                          ("LA", 128 * n + l0, 128 * n + l0 + w), b % 2)
             if t < ST - 1:
                 for h in range(2):
-                    out.append(("ra%d%d%d" % (g, t, h), 1, ("SA", (2 * s + h) * 72, (2 * s + h) * 72 + 72),
-                                ("LA", (2 * s + 2 + h) * 72, (2 * s + 2 + h) * 72 + 72), h))
-                out.append(("rb%d%d" % (g, t), 1, ("SBB", s * 256, s * 256 + 256), ("LB", (s + 1) * 256, (s + 1) * 256 + 256), 2))
-            else:
-                for h in range(2):
-                    out.append(("re%d%d" % (g, h), N - 3, ("SA", (2 * s + h) * 72, (2 * s + h) * 72 + 64),
-                                ("LE", (2 * g + h) * 64, (2 * g + h) * 64 + 64), h))
-                out.append(("rm%d" % g, N - 3, ("SM", 24 * g, 24 * g + 24), ("LM", 24 * g, 24 * g + 24), 0))
-                out.append(("ro%d" % g, N - 2, ("SO", 16 * g, 16 * g + 16), ("LO", 16 * g, 16 * g + 16), 1))
+                    out["rz%d%d" % (n, h)] = (1, ("DZ", 128 * n + 64 * h, 128 * n + 64 * h + 64),
+                                              ("DZ", 128 * n + 128 + 64 * h, 128 * n + 192 + 64 * h), h)
+        out["rm%d" % g] = (N - ST + 1, ("SM", 24 * g, 24 * g + 24), ("LM", 24 * g, 24 * g + 24), 0)
+        out["ro%d" % g] = (N - ST + 2, ("SO", 16 * g, 16 * g + 16), ("LO", 16 * g, 16 * g + 16), 1)
     return out
 
 
 MSG = messages()
-SEMAPHORES = [m[0] for m in MSG] + ["ls"] + ["dm%d" % i for i in range(8)] + ["p%d" % i for i in range(NPOOL)]
+NPOOL = 150 - len(MSG) - 9
+SEMAPHORES = list(MSG) + ["ls"] + ["dm%d" % i for i in range(8)] + ["p%d" % i for i in range(NPOOL)]
 
 
 def route(src, dst, topo, pick):
@@ -71,11 +90,14 @@ def hop(g, T, topo, a, b, src, land, sem):
 
 
 def relay_program(g, core, T, topo):
-    owner = [c for c in T.cores if c in topo.cores_of(core)]
     total = 0
-    for c in owner:
+    for c in [x for x in T.cores if x in topo.cores_of(core)]:
         r = T.rank_of(c)
-        for sem, on, src, land, pick in MSG:
+        if "sends" not in order_cache:
+            ops, seq, _s = plan(g, c, T, topo)
+            order_cache["sends"] = [ops[k]["msg"] for k in seq if ops[k]["msg"]]
+        for sem in order_cache["sends"]:
+            on, src, land, pick = MSG[sem]
             way = route(c, T.cores[(r + on) % N], topo, pick)
             if len(way) == 3 and way[1] == core:
                 g.wait_ge(T.sem[sem], len(topo.engines(c, core)))
@@ -93,19 +115,20 @@ def bits(lo, hi, step):
     return m
 
 
-class_cache = {}
+span_cache = {}
+order_cache = {}
 
 
-def new_op(P, q, emit, rd, wr, dur, sem=None, amount=1, sdeps=(), lat=0.0):
+def new_op(P, q, emit, rd, wr, dur, sem=None, amount=1, sdeps=(), lat=0.0, msg=None):
     ops, track, banks = P["ops"], P["track"], P["banks"]
     k = len(ops)
     deps = set()
     for acc, isw in [(a, False) for a in rd] + [(a, True) for a in wr]:
         name = acc[0]
         key = (acc[1], acc[2], acc[3] if len(acc) > 3 else 1)
-        if key not in class_cache:
-            class_cache[key] = bits(*key)
-        m = class_cache[key]
+        if key not in span_cache:
+            span_cache[key] = bits(*key)
+        m = span_cache[key]
         W, R = track.setdefault(name, ([], []))
         for mm, o in W:
             if mm & m and o != k:
@@ -122,10 +145,10 @@ def new_op(P, q, emit, rd, wr, dur, sem=None, amount=1, sdeps=(), lat=0.0):
             for o in banks[name]:
                 if o != k and ops[o]["q"] != q:
                     deps.add(o)
-            banks[name][:] = [o for o in banks[name] if ops[o]["q"] == q]
+            banks[name][:] = [o for o in banks[name] if o != k and ops[o]["q"] == q]
             banks[name].append(k)
-    banks_fix = None
-    ops.append({"q": q, "emit": emit, "deps": deps, "sdeps": set(sdeps), "dur": dur, "sem": sem, "amount": amount, "lat": lat})
+    ops.append({"q": q, "emit": emit, "deps": deps, "sdeps": set(sdeps), "dur": dur, "sem": sem, "amount": amount, "lat": lat, "msg": msg,
+                "late": P["late"]})
     return k
 
 
@@ -140,6 +163,7 @@ def order_ops(ops):
     for k in range(n - 1, -1, -1):
         o = ops[k]
         prio[k] = o["dur"] + o["lat"] + wake + max([prio[s] for s in succ[k]] or [0.0])
+    prio = [prio[k] - ops[k]["late"] for k in range(n)]
     left = [len(ops[k]["deps"] | ops[k]["sdeps"]) for k in range(n)]
     ready = {}
     free = {}
@@ -164,6 +188,10 @@ def order_ops(ops):
             else:
                 s = max(free[q], min([ready[x] for x in cand[q]]))
                 k = max([x for x in cand[q] if ready[x] <= s + 1e-9], key=lambda x: (prio[x], -x))
+                for j in cand[q]:
+                    if s < ready[j] < s + ops[k]["dur"] and prio[j] > prio[k]:
+                        if max(ready[j] + prio[j], ready[j] + ops[j]["dur"] + prio[k]) < max(s + prio[k], s + ops[k]["dur"] + prio[j]):
+                            s, k = ready[j], j
             if best is None or s < best[0]:
                 best = (s, k, q)
         s, k, q = best
@@ -177,7 +205,7 @@ def order_ops(ops):
             ready[c] = max(ready.get(c, 0.0), fin[k] + wake)
             if left[c] == 0:
                 cand[ops[c]["q"]].append(c)
-    return seq, max(fin)
+    return seq
 
 
 def emit_ops(g, T, ops, seq):
@@ -235,12 +263,18 @@ def emit_ops(g, T, ops, seq):
 
 
 def rank_program(g, core, T, topo):
-    rank = T.rank_of(core)
-    if rank is None:
+    if T.rank_of(core) is None:
         relay_program(g, core, T, topo)
         return
-    P = {"ops": [], "track": {}, "banks": {"b%d" % i: [] for i in range(8)}}
-    C = 0.00095
+    ops, seq, sent = plan(g, core, T, topo)
+    emit_ops(g, T, ops, seq)
+    g.wait_ge(T.sem["ls"], sent[0])
+
+
+def plan(g, core, T, topo):
+    rank = T.rank_of(core)
+    P = {"late": 0.0, "ops": [], "track": {}, "banks": {"b%d" % i: [] for i in range(8)}}
+    C, CP, FAR = 0.0009, 0.0006, FARUS
 
     def ap(a):
         if len(a) > 3:
@@ -289,225 +323,311 @@ def rank_program(g, core, T, topo):
     def fill(out, c):
         new_op(P, "V", lambda: g.vector.memset(ap(out), c), [], [out], vdur(width(out), 1))
 
-    def act(out, in_, func, accum=None, **kw):
+    def act(out, in_, func, off=None, accum=None, **kw):
         def e():
-            if accum is None:
-                return g.scalar.activation(out=ap(out), in_=ap(in_), func=func, **kw)
-            return g.scalar.activation(out=ap(out), in_=ap(in_), func=func, accum_out=ap(accum), **kw)
-        new_op(P, "S", e, [in_], [out] + cols(accum), 0.05 + C * width(out))
+            src = ap(in_) if off is None else ap(in_).indirect(ap(off))
+            more = {k: val(kw[k]) for k in kw}
+            if accum is not None:
+                more["accum_out"] = ap(accum)
+            return g.scalar.activation(out=ap(out), in_=src, func=func, **more)
+        dur = 0.05 + C * max(64, width(out)) if off is None else 0.065 + 1.6 * C * width(out)
+        new_op(P, "S", e, [in_] + cols(off, *kw.values()), [out] + cols(accum), dur)
 
-    def mms(out, pairs):
+    def move(q, out, in_):
+        if q == "V":
+            copy(out, in_)
+        else:
+            act(out, in_, AF.Copy)
+
+    def mms(*groups):
         def e():
             ins = None
-            for i, (l, r) in enumerate(pairs):
-                ins = g.tensor.matmul(ap(out), ap(l), ap(r), i == 0, i == len(pairs) - 1)
+            for out, pairs in groups:
+                for i, (l, r) in enumerate(pairs):
+                    ins = g.tensor.matmul(ap(out), ap(l), ap(r), i == 0, i == len(pairs) - 1)
             return ins
-        f = 4 if SB[pairs[0][0][0]][1] == F32 else 1
-        new_op(P, "P", e, [x for p in pairs for x in p], [out], 0.02 + len(pairs) * C * f * max(64, width(out)))
+        dur = 0.02
+        for out, pairs in groups:
+            dur += len(pairs) * CP * (4 if SB[pairs[0][0][0]][1] == F32 else 1) * max(64, width(out))
+        new_op(P, "P", e, [x for o, pairs in groups for p in pairs for x in p], [o for o, pairs in groups], dur)
 
     def iota(out, pattern, base, cm):
         new_op(P, "G", lambda: g.iota(ap(out), pattern, base, cm), [], [out], 0.13 + 2 * C * width(out))
 
-    def load(q, out, name, sem):
+    loads = []
+
+    def load(q, out, name, sem, lat, also=()):
         eng = g.sync if q == "Y" else g.scalar
-        new_op(P, q, lambda: eng.dma_start(out=ap(out), in_=T[name][:, :]), [], [out], 0.1, sem=sem, amount=16, lat=3.0)
+        loads.append(new_op(P, q, lambda: eng.dma_start(out=ap(out), in_=T[name][:, :]), [], [out] + list(also), 0.1, sem=sem, amount=16,
+                            lat=lat, sdeps=loads[-1:]))
 
     def store(name, in_, sem):
         new_op(P, "Y", lambda: g.sync.dma_start(out=T[name][:, :], in_=ap(in_)), [in_], [], 0.1, sem=sem, amount=16, lat=2.0)
 
     sent = [0]
-    by = {m[0]: m for m in MSG}
 
-    def send(sem):
-        m = by[sem]
-        way = route(core, T.cores[(rank + m[1]) % N], topo, m[4])
+    sends = {}
+
+    def send(sem, after=(), lat=0.0):
+        on, src, land, pick = MSG[sem]
+        way = route(core, T.cores[(rank + on) % N], topo, pick)
 
         def e():
-            sent[0] += hop(g, T, topo, core, way[1], m[2], m[3], sem)
-        k = new_op(P, "G", e, [m[2]], [], 1.0)
-        back = T.cores[(rank - m[1]) % N]
-        cnt = len(topo.engines(route(back, core, topo, m[4])[-2], core))
-        new_op(P, "recv", None, [], [m[3]], 0.0, sem=sem, amount=cnt, sdeps=(k,), lat=4.0)
+            sent[0] += hop(g, T, topo, core, way[1], src, land, sem)
+        k = new_op(P, "G", e, [src], [], 0.5, msg=sem, sdeps=[sends[x] for x in after], lat=lat)
+        sends[sem] = k
+        back = T.cores[(rank - on) % N]
+        cnt = len(topo.engines(route(back, core, topo, pick)[-2], core))
+        new_op(P, "recv", None, [], [land], 0.0, sem=sem, amount=cnt, sdeps=(k,), lat=FAR)
 
-    def sl(name, i, w, lo=0, hi=None, step=1):
-        hi = w if hi is None else hi
-        if step == 1:
-            return (name, i * w + lo, i * w + hi)
-        return (name, i * w + lo, i * w + hi, step)
+    def sl(name, at, lo, hi, step=1):
+        return (name, at + lo, at + hi) if step == 1 else (name, at + lo, at + hi, step)
 
-    def C16F(r): return ("CRF", 128 * r, 128 * r + 128)
-    def C16B(r): return ("CRB", 128 * r, 128 * r + 128)
-    NBWIN, GWIN, XWIN, XALL = ("NBW", 0, 1152), ("GW", 0, 1152), ("XT", 0, 2048), ("XT", 0, 2176)
-    full = lambda n: (n, 0, SB[n][0])
+    def mat(name, r):
+        return (name, 128 * r, 128 * r + 128)
 
-    load("Y", NBWIN, "nb", "dm0")
-    load("S", GWIN, "gn", "dm1")
-    load("Y", full("A0"), "a0", "dm2")
-    load("S", full("TH"), "th", "dm3")
-    load("Y", XWIN, "x", "dm4")
+    def full(name):
+        return (name, 0, SB[name][0])
+
+    def sixteen(name, buf, lo, hi):
+        return [(mat(name, r), (buf, lo + r, hi, 16)) for r in range(16)]
+
+    GWIN, XWIN, NB0, IDM = full("GW"), ("XT", 0, 2049), ("NBR", 0, 1152), full("ID")
+
+    load("Y", NB0, "nb", "dm0", LOADS[0])
+    load("Y", GWIN, "gn", "dm1", LOADS[1])
+    load("Y", ("XT", 1, 2049), "x", "dm4", LOADS[2], also=[("XT", 0, 1)])
+    load("Y", full("A0"), "a0", "dm2", LOADS[3])
+    load("Y", full("TH"), "th", "dm3", LOADS[3])
+    fill(("XT", 0, 1), 0.0)
     iota(full("PI"), [[1, 1]], 0, 1)
     iota(full("MI"), [[1, 128]], 0, 0)
     iota(full("C16"), [[16, 8]], 0, 0)
-    iota(full("DI"), [[-1, 64]], 64, 1)
+    iota(full("WI"), [[1, 32]], 142, -1)
+    iota(full("RI"), [[1, 128]], 128, -1)
+    iota(("IOTA", 0, 1152), [[1, 1152]], -1, 0)
+    iota(("IOTA", 1152, 2064), [[1, 912]], 1151, 0)
     ts(full("PS"), full("PI"), 4, OP.arith_shift_right)
     ts(full("PL"), full("PI"), 15, OP.bitwise_and)
     copy(full("PSF"), full("PS"))
     copy(full("PLF"), full("PL"))
+    ts(full("PL1"), full("PL"), 1.0, OP.add)
+    ts(full("PLM"), full("PL"), -1.0, OP.add)
+    ts(full("PNF"), full("PL1"), 16.0, OP.is_lt, full("PL1"), OP.mult)
+    ts(full("C1S"), full("PNF"), 1152.0, OP.mult)
+    ts(full("ROWM"), full("PL"), 4.0, OP.is_ge)
     ts(full("ILF"), full("C16"), full("PLF"), OP.add)
-    fill(full("HU0"), 0)
-    for h in range(2):
-        ts(("HU0", 8 * h, 8 * h + 4), ("ILF", 4 * h, 4 * h + 4), 9.0, OP.mult)
-    ts(full("DI2"), full("DI"), 15, OP.bitwise_and)
-    copy(full("DELT"), full("DI2"))
+    ts(("L0", 0, 8), full("ILF"), 9.0, OP.mult)
+    fill(("L0", 8, 16), 1)
     ts(full("MS"), full("MI"), 4, OP.arith_shift_right)
     ts(full("ML"), full("MI"), 15, OP.bitwise_and)
     ts(full("ML1"), full("ML"), 1.0, OP.add)
     ts(full("BLK"), full("MS"), full("PSF"), OP.is_equal)
     tt(full("Z"), full("ML1"), full("BLK"), OP.mult)
+    ts(IDM, full("Z"), full("PL1"), OP.is_equal)
+    ts(full("ZD"), IDM, full("PL1"), OP.mult)
     for r in range(16):
-        ts(C16F(r), full("Z"), float(r + 1), OP.is_equal)
+        ts(mat("DIAG", r), full("ZD"), float(r + 1), OP.is_equal)
     for r in range(16):
-        ts(C16B(r), full("Z"), float(r + 1), OP.is_equal)
-    ts(full("PL1"), full("PLF"), 1.0, OP.add)
-    ts(full("IDB"), full("Z"), full("PL1"), OP.is_equal)
-    ts(full("F2"), full("Z"), full("PL1"), OP.is_gt, 2.0, OP.mult)
-    tt(full("FIRST"), full("F2"), full("IDB"), OP.add)
+        ts(mat("CRF", r), full("Z"), float(r + 1), OP.is_equal)
+    ts(full("RJ"), full("RI"), 15, OP.bitwise_and)
+    ts(full("RK"), full("RJ"), 1.0, OP.add)
+    tt(full("ZR"), full("RK"), full("BLK"), OP.mult)
+    for r in range(1, 16):
+        ts(mat("ROT", r), full("ZR"), float(r + 1), OP.is_equal)
+    ts(full("ID2"), IDM, 2.0, OP.mult)
+    tt(full("FM"), full("BLK"), full("ID2"), OP.subtract)
+    act(full("FH"), full("FM"), AF.Copy, scale=0.5)
+    act(full("NEG3"), mat("CRF", ST - 1), AF.Copy, scale=-1.0)
+    act(full("IDB"), IDM, AF.Copy)
+    ts(full("IDR"), IDM, full("ROWM"), OP.mult)
     ts(full("TRI"), full("Z"), full("PL1"), OP.is_gt)
-    ts(full("F4"), full("PLF"), -1.0, OP.mult, 4.0, OP.add)
-    ts(full("ROWM"), full("PLF"), 4.0, OP.is_ge)
     fill(full("ALL"), 0.0625)
     fill(full("ZER"), 0.0)
-    ts(full("NINE"), full("ILF"), 9.0, OP.mult)
-    ts(full("KC"), full("ILF"), -9.0, OP.mult, 1280.0, OP.add)
-    ts(full("B16"), full("ILF"), 16.0, OP.mult)
-    for s in range(4):
-        h = s & 1
-        ts(sl("FBT", s, 8, 0, 4), ("ILF", 4 * h, 4 * h + 4), 2048.0, OP.add)
+    fill(full("ONES"), 1.0)
+    ts(full("KC"), full("ILF"), -1.0, OP.mult, 31.0, OP.add)
+    ts(full("WJ"), full("WI"), 15, OP.bitwise_and)
+    ts(full("WM"), full("WJ"), 0.0, OP.not_equal, 2.0, OP.mult)
+    new_op(P, "V", lambda: g.vector.tensor_tensor_scan(out=ap(("WT", 0, 32)), data0=ap(full("WM")), data1=ap(("ONES", 0, 32)), initial=1.0,
+                                                       op0=OP.mult, op1=OP.max), [full("WM"), ("ONES", 0, 32)], [("WT", 0, 32)], 0.1)
+    act(("WT", 0, 16), ("WT", 16, 32), AF.Copy)
+    w = 32
+    while w < 2080:
+        m = min(w, 2080 - w)
+        act(("WT", w, w + m), ("WT", 0, m), AF.Copy)
+        w += m
+    fill(full("BASE"), 0.0)
+    fill(full("BASE3"), 0.0)
+    for b, (l0, w) in enumerate(BATCH):
+        c0, c = l0 // 16, w // 16
+        for par in range(3):
+            ts(sl("BASE", 32 * par + 4 * c0, c, 2 * c), ("ILF", c0, c0 + c), 16.0, OP.mult, 1.0, OP.add)
+        ts(sl("BASE", 4 * c0, 2 * c, 3 * c), ("ILF", c0, c0 + c), 9.0, OP.mult)
+        ts(sl("BASE3", 2 * c0, 0, c), ("ILF", c0, c0 + c), 16.0, OP.mult, 1.0, OP.add)
     copy(("LIM", 0, 1), full("TH"))
+    act(full("NBF"), NB0, AF.Copy)
+    spare = ["b2", "b5", "b6", "b7"]
+    for j, lo in enumerate(range(1152, 16 * 1152, 512)):
+        hi = min(lo + 512, 16 * 1152)
+        bank = spare[j % 4]
+        cut = [lo] + [x for x in range(1152, 16 * 1152, 1152) if lo < x < hi] + [hi]
+        mms(*[((bank, x - lo, y - lo), [(mat("ROT", x // 1152), ("NBF", x % 1152, x % 1152 + y - x))]) for x, y in zip(cut, cut[1:])])
+        move(EVAC[j % len(EVAC)], ("NBR", lo, hi), (bank, 0, hi - lo))
 
     for gen in range(GENS):
-        ts(full("DZ"), ("GW", 0, 1152, 9), full("ROWM"), OP.mult)
+        n0 = gen * ST
+        act(("DZ", 128 * n0, 128 * n0 + 128), ("GW", 0, 1152, 9), AF.Copy)
+        act(("OW", 0, 128), ("GW", 0, 1152, 9), AF.Copy)
+        for h in range(2):
+            send("rz%d%d" % (n0, h), lat=6.0 if gen == 0 else 0.0)
         for t in range(ST):
-            n = gen * ST + t
+            n = n0 + t
             end = t == ST - 1
-            for h in range(2):
-                s4 = 2 * (n & 1) + h
-                b = ["b%d" % (4 * h + i) for i in range(4)]
-                la = (2 * n + h) * 72
+            par = 0 if t == 0 else 1 + (n & 1)
+            places = []
+            for b, (l0, w) in enumerate(BATCH):
+                c0, c = l0 // 16, w // 16
+                P["late"] = LATE * b
+                bA, bB, bC = ["b%d" % (3 * (b % 2) + i) for i in range(3)]
+                if n == 0:
+                    bC = bA
+                o = 2 * (ST - 1 - t)
+                tile = lambda name: (name, l0, l0 + w)
+                ptile = lambda name: (name, 128 * par + l0, 128 * par + l0 + w)
+                wide = lambda name, lo, hi, step=1: sl(name, 16 * l0, lo, hi, step)
+                ghm = ("GHM", 128 * (n & 1) + l0, 128 * (n & 1) + l0 + w)
                 if t == 0:
-                    hl, ul = ("HU0", 8 * h, 8 * h + 4), ("HU0", 8 * h + 4, 8 * h + 8)
-                    ts(sl("FBT", s4, 8, 4, 8), ("ILF", 4 * h, 4 * h + 4), 9.0, OP.mult)
-                    fill(sl("U1", s4, 4), 1.0)
-                    a = ("A0", 64 * h, 64 * h + 64) if gen == 0 else ("LE", 64 * h, 64 * h + 64)
+                    l1 = l2 = ("L0", c0, c0 + c)
+                    pos, nbw, wtw = ("L0", 8, 8 + c), NB0, ("WT", 0, 32)
+                    a = tile("A0") if gen == 0 else ("LA", 128 * (n - 1) + l0, 128 * (n - 1) + l0 + w)
                 else:
-                    hl, ul = sl("HU", s4, 8, 0, 4), sl("HU", s4, 8, 4, 8)
-                    copy(sl("HU", s4, 8), ("LA", la + 64, la + 72))
-                    copy(sl("FBT", s4, 8, 4, 8), ("LA", la + 64, la + 68))
-                    ts(sl("U1", s4, 4), ("LA", la + 68, la + 72), 1.0, OP.add)
-                    a = ("LA", la, la + 64)
-                gather(sl("D2", s4, 128, 0, 128, 2), full("DELT"), ul)
-                gather(sl("NBG", s4, 64), NBWIN, hl)
-                ts(sl("D2", s4, 128, 1, 128, 2), sl("D2", s4, 128, 0, 128, 2), -8.0, OP.add)
-                for k in range(8):
-                    ts(sl("MASK", s4, 1024, k, 1024, 8), sl("D2", s4, 128), float(k), OP.is_equal)
-                gather2(sl("GHM", s4, 64), GWIN, hl, sl("MASK", s4, 1024, 0, 1024, 16), OP.mult)
-                copy(sl("OFFE", s4, 64), sl("NBG", s4, 64))
-                mms((b[0], 0, 4), [(C16F(r), sl("GHM", s4, 64, r, 64, 16)) for r in range(16)])
-                copy(sl("NL", h, 4), (b[0], 0, 4))
-                gather2(sl("DD", h, 64), XWIN, sl("NL", h, 4), a, OP.subtract)
+                    l1, pos, l2 = lists_at(n, b, o + 2, o + 3), lists_at(n, b, o + 3, o + 4), lists_at(n, b, o + 4, o + 5)
+                    nbw, wtw = full("NBR"), ("WT", 0, 2064)
+                    a = ("LA", 128 * (n - 1) + l0, 128 * (n - 1) + l0 + w)
+                nl = lists_at(n, b, o + 4, o + 5)
+                base = sl("BASE", 32 * par + 4 * c0, 0, 4 * c)
+                if n != ST:
+                    gather(ptile("OFF"), nbw, l1)
+                    act(ptile("WW"), wtw, AF.Copy, off=pos)
+                    ts(ptile("M0"), ptile("WW"), 32768.0, OP.is_ge)
+                    if not end:
+                        act(ptile("HT"), ("IOTA", 0, 1152), AF.Identity, off=l2, bias=1.0)
+                        gather2(ptile("DH"), nbw, l1, ptile("HT"), OP.subtract)
+                if t and not end:
+                    copy(sl("BASE", 32 * par + 4 * c0, 2 * c, 3 * c), l2)
+                ch = 16 * w // len(GGQ)
+                for j, lo in enumerate(range(0, 16 * w, ch)):
+                    off = sl("OFF", 128 * par + l0, lo // 16, (lo + ch) // 16)
+                    if GGQ[j] == "S":
+                        act(wide("GG", lo, lo + ch), GWIN, AF.Copy, off=off)
+                    else:
+                        gather(wide("GG", lo, lo + ch), GWIN, off)
+                ep = (bA, 0, w)
+                mms((ep, [(IDM, ("ONES", 0, w))] + sixteen("DIAG", "GG", 16 * l0, 16 * l0 + 16 * w)))
+                copy(tile("EL"), ep)
+                gather2(ghm, GWIN, l2, ptile("M0"), OP.mult)
+                mms(((bB, 256, 256 + c), [(IDM, ("ONES", 0, c))] + sixteen("CRF", "GHM", ghm[1], ghm[2])))
+                copy(nl, (bB, 256, 256 + c))
+                gather2(tile("DD"), XWIN, nl, a, OP.subtract)
                 for j in range(2):
-                    act(sl("T2", h, 128, j, 128, 2), sl("DD", h, 64), AF.Abs)
+                    act(sl("T2", 2 * l0, j, 2 * w, 2), tile("DD"), AF.Abs)
                 for k in range(8):
-                    act(sl("TEXP", h, 1024, k, 1024, 8), sl("T2", h, 128), AF.Copy)
-                act(("XT", 2048 + 64 * h, 2112 + 64 * h), sl("DD", h, 64), AF.Abs)
-                gather2(sl("GG", h, 1024), GWIN, sl("OFFE", s4, 64), sl("MASK", s4, 1024), OP.mult)
-                mms((b[1], 0, 64), [(C16F(k), sl("GG", h, 1024, k, 1024, 16)) for k in range(16)])
-                copy(sl("EL", h, 64), (b[1], 0, 64))
-                for q in range(2):
-                    gather2(sl("UU", h, 1024, 512 * q, 512 * q + 512), XWIN, sl("EL", h, 64, 32 * q, 32 * q + 32),
-                            sl("TEXP", h, 1024, 512 * q, 512 * q + 512), OP.add)
-                    act(sl("AB", h, 1024, 512 * q, 512 * q + 512), sl("UU", h, 1024, 512 * q, 512 * q + 512), AF.Abs, bias=-255.0)
-                mms((b[2], 0, 64), [(C16B(k), sl("AB", h, 1024, k, 1024, 16)) for k in range(16)])
-                ts(sl("OKT", h, 64), (b[2], 0, 64), ("LIM", n, n + 1), OP.is_le)
-                mms((b[2], 0, 64), [(full("FIRST"), sl("OKT", h, 64))])
-                sel = sl("PACK", h, 320, 128, 192)
-                ts(sel, (b[2], 0, 64), 1.0, OP.is_equal)
-                ts(sl("PACK", h, 320, 192, 256), (b[2], 0, 64), 1.0, OP.is_equal)
-                ts(sl("PACK", h, 320, 256, 320), (b[2], 0, 64), 1.0, OP.is_equal, full("PLF"), OP.mult)
-                tt(sl("PACK", h, 320, 0, 64), sel, (b[1], 0, 64), OP.mult)
-                tt(sl("PACK", h, 320, 64, 128), sel, sl("NBG", s4, 64), OP.mult)
-                mms((b[0], 0, 20), [(C16F(r), sl("PACK", h, 320, r, 320, 16)) for r in range(16)])
-                ts(sl("NF", h, 8), (b[0], 8, 16), -1.0, OP.mult, 1.0, OP.add)
-                tt(sl("TMP", h, 8), sl("NF", h, 8), sl("FBT", s4, 8), OP.mult)
-                tt(sl("IDXF", h, 4), sl("TMP", h, 8, 0, 4), (b[0], 0, 4), OP.add)
-                copy(sl("IDX", h, 4), sl("IDXF", h, 4))
-                sa = (2 * n + h) * 72
+                    move(EXPQ[k], wide("TEXP", k, 16 * w, 8), sl("T2", 2 * l0, 0, 2 * w))
+                for lo in range(0, 16 * w, GCH):
+                    gather2(wide("UU", lo, lo + GCH), XWIN, sl("EL", l0, lo // 16, (lo + GCH) // 16), wide("TEXP", lo, lo + GCH), OP.add)
+                    act(wide("AB", lo, lo + GCH), wide("UU", lo, lo + GCH), AF.Abs, bias=-255.0)
+                mms(((bB, 0, w), sixteen("CRF", "AB", 16 * l0, 16 * l0 + 16 * w)))
+                ts(tile("OK"), (bB, 0, w), ("LIM", n, n + 1), OP.is_le)
+                tt(tile("OKW"), tile("OK"), ptile("WW"), OP.mult)
+                fs, fe, tot = (bB, 64, 64 + w), (bB, 128, 128 + w), (bC, 64, 64 + w)
+                mms((fs, [(full("FM"), tile("OKW"))]), (fe, [(full("FH"), ptile("M0")), (full("FM"), tile("OKW"))]))
+                mms((tot, [(full("BLK"), tile("OKW"))]))
+                act(tile("NF"), tot, AF.Relu, accum=("RF", b, b + 1), scale=-1.0, bias=1.0)
+                pk = lambda j: sl("PACK", 4 * l0, j * w, j * w + w)
+                ts(tile("SEL"), fs, 0.0, OP.is_lt)
+                sa = ("SA", 128 * n + l0, 128 * n + l0 + w)
                 if not end:
-                    tt(("SA", sa + 64, sa + 68), sl("TMP", h, 8, 4, 8), (b[0], 4, 8), OP.add)
-                tt(("SA", sa + 68, sa + 72), sl("U1", s4, 4), (b[0], 16, 20), OP.add)
-                gather(("SA", sa, sa + 64), XALL, sl("IDX", h, 4))
-                send("re%d%d" % (gen, h) if end else "ra%d%d%d" % (gen, t, h))
-                mms((b[3], 0, 64), [(full("BLK"), sel)])
-                act(sl("NFB", h, 64), (b[3], 0, 64), AF.Identity, accum=("RF", h, h + 1), scale=-1.0, bias=1.0)
-                fo = ("SBB", 256 * n + 128 + 64 * h, 256 * n + 192 + 64 * h)
-                if t == 0:
-                    copy(fo, (b[3], 0, 64))
+                    tt(pk(2), tile("SEL"), ptile("DH"), OP.mult)
+                    tt(pk(3), tile("SEL"), ep, OP.mult)
+                    ts(pk(0), fe, 0.0, OP.is_lt, full("C1S"), OP.mult)
+                    ts(pk(1), fe, 0.0, OP.is_lt, full("PNF"), OP.mult)
+                    mms(((bB, 320, 320 + 4 * c), [(IDM, base)] + sixteen("CRF", "PACK", 4 * l0, 4 * l0 + 4 * w)))
+                    copy(lists_at(n, b, o + 1, o + 4), (bB, 320 + c, 320 + 4 * c))
+                    new = lists_at(n, b, o, o + 1)
+                    for j in range(c):
+                        ts(("H", new[1] + j, new[1] + j + 1), (bB, 320 + j, 321 + j), (bB, 320 + 2 * c + j, 321 + 2 * c + j), OP.add)
+                    send("rl%d%d" % (n, b), after=["rz%d%d" % (n, h) for h in range(2) if t == 0])
+                    place, idx, pe = lists_at(n, b, o + 1, o + 2), lists_at(n, b, o + 3, o + 4), pk(3)
                 else:
-                    tt(fo, ("LB", 256 * n + 128 + 64 * h, 256 * n + 192 + 64 * h), (b[3], 0, 64), OP.add)
-                tt(sl("GHF", h, 64), sl("GHM", s4, 64), sl("NFB", h, 64), OP.mult)
-                mms((b[3], 64, 128), [(C16F(t), sl("PACK", h, 320, 0, 64)), (C16F(t), sl("GHF", h, 64))])
-                prev = ("DZ", 64 * h, 64 * h + 64) if t == 0 else ("LB", 256 * n + 64 * h, 256 * n + 64 * h + 64)
-                tt(("SBB", 256 * n + 64 * h, 256 * n + 64 * h + 64), prev, (b[3], 64, 128), OP.add)
-            if not end:
-                send("rb%d%d" % (gen, t))
-            for h in range(2):
-                sa = (2 * n + h) * 72
-                copy(("UI", 4 * h, 4 * h + 4), ("SA", sa + 68, sa + 72))
-            ts(full("UI2"), full("UI"), 15, OP.bitwise_and)
-            tt(full("UI3"), full("UI2"), full("B16"), OP.add)
-            copy(full("POS"), full("UI3"))
-            for h in range(2):
-                sa = (2 * n + h) * 72
-                scatter(XWIN, ("POS", 4 * h, 4 * h + 4), ("SA", sa, sa + 64))
+                    tt(pk(1), tile("SEL"), ep, OP.mult)
+                    ts(pk(0), fe, 0.0, OP.is_lt, full("PNF"), OP.mult)
+                    mms(((bB, 320, 320 + 2 * c), [(IDM, sl("BASE3", 2 * c0, 0, 2 * c))] + sixteen("CRF", "PACK", 4 * l0, 4 * l0 + 2 * w)))
+                    copy(sl("EN", 2 * c0, 0, 2 * c), (bB, 320, 320 + 2 * c))
+                    place, idx, pe = sl("EN", 2 * c0, 0, c), sl("EN", 2 * c0, c, 2 * c), pk(1)
+                tt(tile("NFT"), tile("NF"), sl("T2", 2 * l0, 0, 2 * w, 2), OP.mult)
+                gather2(sa, XWIN, idx, tile("NFT"), OP.add)
+                send("ra%d%d" % (n, b))
+                places.append((place, sa))
+                if end:
+                    hl = lambda name, lo, hi: sl(name, 6 * c0, lo * c, hi * c)
+                    copy(hl("HF", 0, 6), lists_at(n, b, 5, 11))
+                    ts(hl("HZ", 0, 6), hl("HF", 0, 6), 0.0, OP.is_equal)
+                    tt(hl("HM", 0, 5), hl("HZ", 0, 5), hl("HF", 1, 6), OP.mult)
+                    tt(hl("HV", 0, 5), hl("HM", 0, 5), hl("HF", 0, 5), OP.add)
+                    copy(hl("VL", 0, 5), hl("HV", 0, 5))
+                    tt(("E1", c0, c0 + c), hl("HZ", 0, 1), hl("HZ", 2, 3), OP.add)
+                    tt(("E2", c0, c0 + c), ("E1", c0, c0 + c), hl("HZ", 4, 5), OP.add)
+                    copy(("EU", c0, c0 + c), ("E2", c0, c0 + c))
+                    act(tile("CM"), ("IOTA", 0, 16), AF.Identity, off=("EU", c0, c0 + c), scale=-1.0, bias=full("PLM"))
+                    for j in range(ST - 1):
+                        act(sl("VT", 128 * j, l0, l0 + w), ("IOTA", 0, 2049), AF.Copy, off=hl("VL", 4 - 2 * j, 5 - 2 * j))
+                    tt(tile("IND"), tile("NF"), tile("CM"), OP.is_equal)
+                    tt(tile("GHF"), tile("NF"), ghm, OP.mult)
+                    mms((("b6", l0, l0 + w), [(full("IDR"), ("DZ", 128 * n + l0, 128 * n + l0 + w))]
+                         + [(mat("DIAG", j), sl("VT", 128 * j, l0, l0 + w)) for j in range(ST - 1)]
+                         + [(mat("CRF", t), pe), (mat("CRF", t), tile("GHF")), (full("NEG3"), tile("SEL"))]))
+                    act(tile("DT"), ("b6", l0, l0 + w), AF.Copy)
+            P["late"] = 0.0
+            if t < ST - 2:
+                for h in range(2):
+                    send("rz%d%d" % (n + 1, h), after=["ra%d%d" % (n, NBAT - 1)])
+            for place, sa in places:
+                scatter(XWIN, place, sa)
             if n < GENS * ST - 1:
-                mms(("b3", 128, 129), [(full("ALL"), ("RF", 0, 1)), (full("ALL"), ("RF", 1, 2))])
-                copy(full("AI"), ("b3", 128, 129))
+                mms(((bC, 128, 129), [(full("ALL"), ("RF", b, b + 1)) for b in range(NBAT)]))
+                copy(full("AI"), (bC, 128, 129))
                 ts(full("AI2"), full("AI"), 63, OP.bitwise_and)
                 tt(("LIM", n + 1, n + 2), full("AI2"), full("TH"), OP.add)
-        n = gen * ST + ST - 1
-        ts(full("IND"), ("SBB", 256 * n + 128, 256 * n + 256), full("F4"), OP.is_equal)
         new_op(P, "V", lambda: g.vector.tensor_reduce(out=ap(full("NRED")), in_=ap(full("IND")), axis=AxisListType.X, op=OP.add),
-               [full("IND")], [full("NRED")], 0.15)
-        mms(("b0", 32, 33), [(full("TRI"), full("NRED"))])
+               [full("IND")], [full("NRED")], 0.13)
+        mms((("b7", 0, 1), [(full("TRI"), full("NRED"))]))
         new_op(P, "V", lambda: g.vector.tensor_tensor_scan(out=ap(full("PRE")), data0=ap(full("ZER")), data1=ap(full("IND")),
-                                                           initial=ap(("b0", 32, 33)), op0=OP.add, op1=OP.add),
-               [full("IND"), full("ZER"), ("b0", 32, 33)], [full("PRE")], 0.15)
+                                                           initial=ap(("b7", 0, 1)), op0=OP.add, op1=OP.add),
+               [full("IND"), full("ZER"), ("b7", 0, 1)], [full("PRE")], 0.13)
         tt(full("PPK"), full("PRE"), full("IND"), OP.mult)
-        mms(("b4", 0, 8), [(C16F(r), ("PPK", r, 128, 16)) for r in range(16)])
-        ts(full("POSL"), ("b4", 0, 8), -1.0, OP.add)
-        scatter(full("SD"), full("POSL"), ("SBB", 256 * n, 256 * n + 128))
-        copy(("SM", 24 * gen + 8, 24 * gen + 24), ("SD", 0, 32, 2))
-        copy(("SO", 16 * gen, 16 * gen + 16), ("SD", 1, 32, 2))
-        ts(full("GEC"), ("b4", 0, 8), 97.0, OP.is_ge)
-        tt(full("DQ"), full("KC"), ("b4", 0, 8), OP.subtract)
+        q1 = ("b7", 16, 24)
+        mms((q1, sixteen("CRF", "PPK", 0, 128)))
+        ts(full("POSL"), q1, -1.0, OP.mult, 128.0, OP.add)
+        scatter(full("SD"), full("POSL"), full("DT"))
+        copy(("SM", 24 * gen + 8, 24 * gen + 24), ("SD", 97, 128, 2))
+        act(("SO", 16 * gen, 16 * gen + 16), ("SD", 96, 128, 2), AF.Copy)
+        ts(full("GEC"), q1, 97.0, OP.is_ge)
+        tt(full("DQ"), full("KC"), q1, OP.add)
         tt(full("MLQ"), full("GEC"), full("DQ"), OP.mult)
-        tt(("SM", 24 * gen, 24 * gen + 8), full("MLQ"), full("NINE"), OP.add)
-        send("rm%d" % gen)
+        tt(("SM", 24 * gen, 24 * gen + 8), full("MLQ"), full("ILF"), OP.add)
         send("ro%d" % gen)
+        send("rm%d" % gen)
         copy(full("IDN"), ("LM", 24 * gen, 24 * gen + 8))
-        copy(("GW", 1152, 1184, 2), ("LM", 24 * gen + 8, 24 * gen + 24))
-        copy(("GW", 1153, 1184, 2), ("LO", 16 * gen, 16 * gen + 16))
-        gather(full("NEW"), ("GW", 0, 1184), full("IDN"))
-        if gen < GENS - 1:
-            copy(("GW", 0, 1152, 9), full("NEW"))
+        act(("OW", 129, 160, 2), ("LM", 24 * gen + 8, 24 * gen + 24), AF.Copy)
+        act(("OW", 128, 160, 2), ("LO", 16 * gen, 16 * gen + 16), AF.Copy)
+        gather(("GW", 0, 1152, 9) if gen < GENS - 1 else full("NEW"), full("OW"), full("IDN"))
     store("yg", full("NEW"), "dm5")
-    for h in range(2):
-        copy(("YA", 64 * h, 64 * h + 64), ("LE", 128 + 64 * h, 192 + 64 * h))
+    act(full("YA"), ("LA", 128 * (GENS * ST - 1), 128 * GENS * ST), AF.Copy)
     store("ya", full("YA"), "dm6")
-    mms(("b7", 0, 128), [(full("IDB"), ("XT", j, 2048, 16)) for j in range(16)])
-    copy(full("YS"), ("b7", 0, 128))
+    mms((("b5", 0, 128), [(full("IDB"), ("XT", 1 + j, 2049, 16)) for j in range(16)]))
+    act(full("YS"), ("b5", 0, 128), AF.Copy)
     store("ys", full("YS"), "dm7")
 
-    seq, total = order_ops(P["ops"])
-    emit_ops(g, T, P["ops"], seq)
-    g.wait_ge(T.sem["ls"], sent[0])
+    if "seq" not in order_cache:
+        order_cache["seq"] = order_ops(P["ops"])
+    return P["ops"], order_cache["seq"], sent

@@ -8,38 +8,56 @@ GENS, ST, N = 2, 4, 8
 BATCH = [(0, 64), (64, 64)]
 NBAT = len(BATCH)
 GCH = 256
+ACH = 256
+TCH = 256
+SUB = 64
 GGQ = "SVSS"
-LOADS = (3.5, 1.5, 1.5, 0.1)
-FARUS = 4.5
-LATE = 3.0
-EXPQ = "VVVVSSSS"
+M0Q = "S"
+WTQ = "V"
 EVAC = "SVSSV"
+LOADS = (3.5, 1.5, 1.5, 0.1)
+FARUS = 3.7
+LATE = 5.0
+BLATE = 0.0
+WAKE = 0.23
+PASSES = 6
+CPE = 0.00043
 HS = 48
 
 F32, F16, BF, I32, U16 = "float32", "float16", "bfloat16", "int32", "uint16"
 SB = {
     "GW": (1152, I32), "NBR": (16 * 1152, I32), "NBF": (1152, F16), "XT": (2064, BF), "A0": (128, BF), "TH": (1, I32),
-    "PI": (1, I32), "PS": (1, I32), "PL": (1, I32), "PSF": (1, F32), "PLF": (1, F32), "PL1": (1, F32), "PN": (1, I32), "PNF": (1, F32),
-    "C1S": (1, F32), "PLM": (1, F32), "ROWM": (1, F32), "MI": (128, I32), "MS": (128, I32), "ML": (128, I32), "ML1": (128, F16),
-    "BLK": (128, F16), "Z": (128, F16), "ZD": (128, F16), "RI": (128, I32), "RJ": (128, I32), "RK": (128, F16), "ZR": (128, F16),
-    "CRF": (2048, F16), "DIAG": (2048, F16), "ROT": (2048, F16), "ID": (128, F16), "ID2": (128, F16), "IDB": (128, BF), "FM": (128, F16), "FH": (128, F16),
-    "NEG3": (128, F16), "IDR": (128, F16), "TRI": (128, F32), "ALL": (128, F32), "ZER": (128, F16), "ONES": (128, F16),
-    "WI": (32, I32), "WJ": (32, I32), "WM": (32, F32), "WT": (2080, BF), "IOTA": (2064, I32), "C16": (8, I32), "ILF": (8, F32),
-    "L0": (16, U16), "KC": (8, F32), "BASE": (4 * 32, F16), "BASE3": (16, F16),
-    "OFF": (3 * 128, U16), "WW": (3 * 128, F16), "M0": (3 * 128, F16), "HT": (3 * 128, F16), "DH": (3 * 128, F16), "GHM": (2 * 128, F16),
-    "DD": (128, BF), "T2": (256, BF), "TEXP": (2048, BF), "GG": (2048, F16), "EL": (128, U16), "UU": (2048, F16), "AB": (2048, F16),
-    "OK": (128, F16), "OKW": (128, F16), "SEL": (128, F16), "PACK": (512, F16), "NF": (128, F16), "NFT": (128, BF), "EN": (16, U16),
-    "RF": (NBAT, F32), "AI": (1, I32), "AI2": (1, I32), "LIM": (9, F32),
-    "HF": (48, F32), "HZ": (48, F32), "HM": (48, F32), "HV": (48, F32), "VL": (48, U16), "E1": (8, F32), "E2": (8, F32), "EU": (8, U16),
-    "CM": (128, F16), "VT": (3 * 128, F16), "GHF": (128, F16), "DT": (128, F16), "IND": (128, F16), "NRED": (1, F32), "PRE": (128, F32),
-    "PPK": (128, F16), "POSL": (8, U16), "SD": (128, F32), "GEC": (8, F32), "DQ": (8, F32), "MLQ": (8, F32), "IDN": (8, U16),
-    "OW": (160, F32), "NEW": (128, F32), "YA": (128, F32), "YS": (128, F32),
+    "PI": (1, I32), "PS": (1, I32), "PL": (1, I32), "PSF": (1, F32), "PLF": (1, F32), "PL1": (1, F32), "PNF": (1, F32), "C1S": (1, F32),
+    "PLM": (1, F32), "ROWM": (1, F32), "WB": (1, F32), "TH1": (1, F32), "C16": (8, I32), "ILF": (8, F32), "KC": (8, F32),
+    "MI": (128, I32), "MS": (128, I32), "ML": (128, I32), "ML1": (128, F16), "RI": (128, I32), "RJ": (128, I32), "RK": (128, F16),
+    "BLK": (128, F16), "BLB": (128, BF), "Z": (128, F16), "ZD": (128, F16), "ZR": (128, F16), "ID": (128, F16), "ID2": (128, F16),
+    "IDB": (128, BF), "IDR": (128, F16), "CRF": (2048, F16), "DIAG": (2048, F16), "ROT": (2048, F16), "FM": (128, F16), "FA": (128, BF),
+    "FB": (128, BF), "FH": (128, BF), "UPR": (128, BF), "NEG3": (128, F16), "TRI": (128, F32), "ALL": (128, F32), "ZER": (128, F16),
+    "ONES": (128, F16), "QTR": (16, F32), "PW": (16, F32), "PW1": (16, F32), "WI": (32, I32), "WJ": (32, I32), "WT": (2080, BF),
+    "IOTA": (2064, I32), "L0": (16, U16), "REPL": (64, U16), "BASE3": (16, F16),
+    "OFF": (3 * 128, U16), "M0": (3 * 128, BF), "HT": (3 * 128, F16), "DH": (3 * 128, F16), "BASE": (3 * 32, F16), "GHM": (2 * 128, F16),
+    "LIMA": (256, F32), "LIMB": (256, F32), "POS": (16, U16),
+    "DD": (128, BF), "TEXP": (2048, BF), "GG": (2048, F16), "EL": (128, U16), "UU": (2048, F16), "AB": (2048, F16), "OK": (128, BF),
+    "OKB": (128, BF), "SEL": (128, F16), "PACK": (512, F16), "NF": (128, F16), "NFT": (128, BF), "EN": (8, U16),
+    "RF": (NBAT, F32), "AI": (1, I32), "AI2": (1, I32), "LIM": (8, F32),
+    "HF": (48, F32), "HZ": (48, F32), "HM": (48, F32), "HV": (48, F32), "VL": (48, U16),
+    "E1": (8, F32), "E2": (8, F32), "EU": (8, U16), "CM": (128, F16), "VT": (3 * 128, F16), "GHF": (128, F16), "DT": (128, F16),
+    "IND": (128, F16), "NRED": (1, F32), "PRE": (128, F32), "PPK": (128, F16), "POSL": (8, U16), "SD": (128, F32),
+    "GEC": (8, F32), "DQ": (8, F32), "MLQ": (8, F32), "IDN": (8, U16), "OW": (160, F32), "NEW": (128, F32), "YA": (128, F32),
+    "YS": (128, F32),
     "H": (GENS * ST * NBAT * HS, U16), "SA": (GENS * ST * 128, BF), "LA": (GENS * ST * 128, BF), "DZ": (GENS * ST * 128, F16),
     "SM": (GENS * 24, F16), "LM": (GENS * 24, F16), "SO": (GENS * 16, F16), "LO": (GENS * 16, F16),
 }
 SCRATCH = {}
+POOLED = {}
 for _n in SB:
-    SCRATCH[_n] = ("sbuf", [128, SB[_n][0]], SB[_n][1])
+    if SB[_n][0] <= 8 and SB[_n][1] in (F32, I32) and _n != "TH":
+        _b = "K" + SB[_n][1]
+        _at = SCRATCH[_b][1][1] if _b in SCRATCH else 0
+        POOLED[_n] = (_b, _at)
+        SCRATCH[_b] = ("sbuf", [128, _at + SB[_n][0]], SB[_n][1])
+    else:
+        SCRATCH[_n] = ("sbuf", [128, SB[_n][0]], SB[_n][1])
 for _i in range(8):
     SCRATCH["b%d" % _i] = ("psum", [128, 512], F32)
 
@@ -129,15 +147,15 @@ def new_op(P, q, emit, rd, wr, dur, sem=None, amount=1, sdeps=(), lat=0.0, msg=N
         if key not in span_cache:
             span_cache[key] = bits(*key)
         m = span_cache[key]
-        W, R = track.setdefault(name, ([], []))
-        for mm, o in W:
+        Wr, R = track.setdefault(name, ([], []))
+        for mm, o in Wr:
             if mm & m and o != k:
                 deps.add(o)
         if isw:
             for mm, o in R:
                 if mm & m and o != k:
                     deps.add(o)
-            W[:] = [(mm & ~m, o) for mm, o in W if mm & ~m] + [(m, k)]
+            Wr[:] = [(mm & ~m, o) for mm, o in Wr if mm & ~m] + [(m, k)]
             R[:] = [(mm & ~m, o) for mm, o in R if mm & ~m]
         else:
             R.append((m, k))
@@ -152,60 +170,55 @@ def new_op(P, q, emit, rd, wr, dur, sem=None, amount=1, sdeps=(), lat=0.0, msg=N
     return k
 
 
+def place_ops(ops, before, after, key, back):
+    n = len(ops)
+    left = [len(before[k]) for k in range(n)]
+    ready, lo_of, hi_of, busy = [0.0] * n, [0.0] * n, [0.0] * n, {}
+    cand = [k for k in range(n) if left[k] == 0]
+    while cand:
+        k = min(cand, key=lambda x: key[x])
+        cand.remove(k)
+        o = ops[k]
+        s, dur = ready[k] + (o["lat"] if back else 0.0), o["dur"]
+        if o["q"] != "recv":
+            taken = busy.setdefault(o["q"], [])
+            at = len(taken)
+            while at > 0 and taken[at - 1][1] > s:
+                at -= 1
+            while at < len(taken) and s + dur > taken[at][0]:
+                s = max(s, taken[at][1])
+                at += 1
+            taken.insert(at, (s, s + dur))
+        lo_of[k], hi_of[k] = s, s + dur
+        for c in after[k]:
+            left[c] -= 1
+            ready[c] = max(ready[c], s + dur + (0.0 if back else o["lat"]) + WAKE)
+            if left[c] == 0:
+                cand.append(c)
+    return lo_of, hi_of
+
+
 def order_ops(ops):
     n = len(ops)
-    wake = 0.06
-    prio = [0.0] * n
+    pred = [ops[k]["deps"] | ops[k]["sdeps"] for k in range(n)]
     succ = [[] for _i in range(n)]
     for k in range(n):
-        for d in ops[k]["deps"] | ops[k]["sdeps"]:
+        for d in pred[k]:
             succ[d].append(k)
+    way = [0.0] * n
     for k in range(n - 1, -1, -1):
-        o = ops[k]
-        prio[k] = o["dur"] + o["lat"] + wake + max([prio[s] for s in succ[k]] or [0.0])
-    prio = [prio[k] - ops[k]["late"] for k in range(n)]
-    left = [len(ops[k]["deps"] | ops[k]["sdeps"]) for k in range(n)]
-    ready = {}
-    free = {}
-    cand = {}
-    for k in range(n):
-        free[ops[k]["q"]] = 0.0
-        cand[ops[k]["q"]] = []
-    for k in range(n):
-        if left[k] == 0:
-            cand[ops[k]["q"]].append(k)
-            ready[k] = 0.0
-    fin = [0.0] * n
-    seq = []
-    while len(seq) < n:
-        best = None
-        for q in cand:
-            if not cand[q]:
-                continue
-            if q == "recv":
-                k = min(cand[q], key=lambda x: ready[x])
-                s = ready[k]
-            else:
-                s = max(free[q], min([ready[x] for x in cand[q]]))
-                k = max([x for x in cand[q] if ready[x] <= s + 1e-9], key=lambda x: (prio[x], -x))
-                for j in cand[q]:
-                    if s < ready[j] < s + ops[k]["dur"] and prio[j] > prio[k]:
-                        if max(ready[j] + prio[j], ready[j] + ops[j]["dur"] + prio[k]) < max(s + prio[k], s + ops[k]["dur"] + prio[j]):
-                            s, k = ready[j], j
-            if best is None or s < best[0]:
-                best = (s, k, q)
-        s, k, q = best
-        cand[q].remove(k)
-        if q != "recv":
-            free[q] = s + ops[k]["dur"]
-        fin[k] = s + ops[k]["dur"] + ops[k]["lat"]
-        seq.append(k)
-        for c in succ[k]:
-            left[c] -= 1
-            ready[c] = max(ready.get(c, 0.0), fin[k] + wake)
-            if left[c] == 0:
-                cand[ops[c]["q"]].append(c)
-    return seq
+        way[k] = ops[k]["dur"] + ops[k]["lat"] + WAKE + max([way[s] for s in succ[k]] or [0.0])
+    key = [(ops[k]["late"] - way[k], k) for k in range(n)]
+    best = None
+    for _i in range(PASSES):
+        lo, hi = place_ops(ops, pred, succ, key, False)
+        total = max(hi[k] + ops[k]["lat"] for k in range(n))
+        if best is None or total < best[0]:
+            best = (total, lo)
+        _l, late = place_ops(ops, succ, pred, [(-hi[k] - ops[k]["lat"], -k) for k in range(n)], True)
+        key = [(-late[k], k) for k in range(n)]
+    order_cache["total"] = best[0]
+    return sorted(range(n), key=lambda k: (best[1][k], k))
 
 
 def emit_ops(g, T, ops, seq):
@@ -274,9 +287,12 @@ def rank_program(g, core, T, topo):
 def plan(g, core, T, topo):
     rank = T.rank_of(core)
     P = {"late": 0.0, "ops": [], "track": {}, "banks": {"b%d" % i: [] for i in range(8)}}
-    C, CP, FAR = 0.0009, 0.0006, FARUS
+    C, CP, FAR = 0.00085, CPE, FARUS
 
     def ap(a):
+        if a[0] in POOLED:
+            name, at = POOLED[a[0]]
+            return T[name][:, at + a[1]:at + a[2]]
         if len(a) > 3:
             return T[a[0]][:, a[1]:a[2]:a[3]]
         return T[a[0]][:, a[1]:a[2]]
@@ -310,6 +326,13 @@ def plan(g, core, T, topo):
         f = 2 if (in0[0] in SB and in1[0] in SB) else 1
         new_op(P, "V", lambda: g.vector.tensor_tensor(out=ap(out), in0=ap(in0), in1=ap(in1), op=op), [in0, in1], [out], vdur(width(out), f))
 
+    def scan(out, data0, data1, initial, op0, op1):
+        new_op(P, "V", lambda: g.vector.tensor_tensor_scan(out=ap(out), data0=ap(data0), data1=ap(data1), initial=val(initial), op0=op0, op1=op1),
+               [data0, data1] + cols(initial), [out], vdur(width(out), 1))
+
+    def add_up(out, in_):
+        new_op(P, "V", lambda: g.vector.tensor_reduce(out=ap(out), in_=ap(in_), axis=AxisListType.X, op=OP.add), [in_], [out], vdur(width(in_), 1))
+
     def gather(out, win, off):
         new_op(P, "V", lambda: g.vector.tensor_copy(out=ap(out), in_=ap(win).indirect(ap(off))), [win, off], [out], 0.05 + 1.6 * C * width(out))
 
@@ -330,7 +353,7 @@ def plan(g, core, T, topo):
             if accum is not None:
                 more["accum_out"] = ap(accum)
             return g.scalar.activation(out=ap(out), in_=src, func=func, **more)
-        dur = 0.05 + C * max(64, width(out)) if off is None else 0.065 + 1.6 * C * width(out)
+        dur = 0.02 + C * max(64, width(out)) if off is None else 0.065 + 1.6 * C * width(out)
         new_op(P, "S", e, [in_] + cols(off, *kw.values()), [out] + cols(accum), dur)
 
     def move(q, out, in_):
@@ -338,6 +361,12 @@ def plan(g, core, T, topo):
             copy(out, in_)
         else:
             act(out, in_, AF.Copy)
+
+    def pick(q, out, win, off):
+        if q == "V":
+            gather(out, win, off)
+        else:
+            act(out, win, AF.Copy, off=off)
 
     def mms(*groups):
         def e():
@@ -365,19 +394,18 @@ def plan(g, core, T, topo):
         new_op(P, "Y", lambda: g.sync.dma_start(out=T[name][:, :], in_=ap(in_)), [in_], [], 0.1, sem=sem, amount=16, lat=2.0)
 
     sent = [0]
-
     sends = {}
 
     def send(sem, after=(), lat=0.0):
-        on, src, land, pick = MSG[sem]
-        way = route(core, T.cores[(rank + on) % N], topo, pick)
+        on, src, land, relay = MSG[sem]
+        way = route(core, T.cores[(rank + on) % N], topo, relay)
 
         def e():
             sent[0] += hop(g, T, topo, core, way[1], src, land, sem)
         k = new_op(P, "G", e, [src], [], 0.5, msg=sem, sdeps=[sends[x] for x in after], lat=lat)
         sends[sem] = k
         back = T.cores[(rank - on) % N]
-        cnt = len(topo.engines(route(back, core, topo, pick)[-2], core))
+        cnt = len(topo.engines(route(back, core, topo, relay)[-2], core))
         new_op(P, "recv", None, [], [land], 0.0, sem=sem, amount=cnt, sdeps=(k,), lat=FAR)
 
     def sl(name, at, lo, hi, step=1):
@@ -394,16 +422,16 @@ def plan(g, core, T, topo):
 
     GWIN, XWIN, NB0, IDM = full("GW"), ("XT", 0, 2049), ("NBR", 0, 1152), full("ID")
 
+    load("S", full("TH"), "th", "dm3", 0.0)
     load("Y", NB0, "nb", "dm0", LOADS[0])
     load("Y", GWIN, "gn", "dm1", LOADS[1])
-    load("Y", ("XT", 1, 2049), "x", "dm4", LOADS[2], also=[("XT", 0, 1)])
+    load("Y", ("XT", 1, 2049), "x", "dm4", LOADS[2], [("XT", 0, 1)])
     load("Y", full("A0"), "a0", "dm2", LOADS[3])
-    load("Y", full("TH"), "th", "dm3", LOADS[3])
     fill(("XT", 0, 1), 0.0)
     iota(full("PI"), [[1, 1]], 0, 1)
     iota(full("MI"), [[1, 128]], 0, 0)
     iota(full("C16"), [[16, 8]], 0, 0)
-    iota(full("WI"), [[1, 32]], 142, -1)
+    iota(full("WI"), [[1, 32]], 127, -1)
     iota(full("RI"), [[1, 128]], 128, -1)
     iota(("IOTA", 0, 1152), [[1, 1152]], -1, 0)
     iota(("IOTA", 1152, 2064), [[1, 912]], 1151, 0)
@@ -412,8 +440,8 @@ def plan(g, core, T, topo):
     copy(full("PSF"), full("PS"))
     copy(full("PLF"), full("PL"))
     ts(full("PL1"), full("PL"), 1.0, OP.add)
-    ts(full("PLM"), full("PL"), -1.0, OP.add)
     ts(full("PNF"), full("PL1"), 16.0, OP.is_lt, full("PL1"), OP.mult)
+    ts(full("PLM"), full("PL"), -1.0, OP.add)
     ts(full("C1S"), full("PNF"), 1152.0, OP.mult)
     ts(full("ROWM"), full("PL"), 4.0, OP.is_ge)
     ts(full("ILF"), full("C16"), full("PLF"), OP.add)
@@ -435,26 +463,33 @@ def plan(g, core, T, topo):
     tt(full("ZR"), full("RK"), full("BLK"), OP.mult)
     for r in range(1, 16):
         ts(mat("ROT", r), full("ZR"), float(r + 1), OP.is_equal)
+    act(full("NEG3"), mat("CRF", ST - 1), AF.Copy, scale=-1.0)
+    fill(full("ZER"), 0.0)
     ts(full("ID2"), IDM, 2.0, OP.mult)
     tt(full("FM"), full("BLK"), full("ID2"), OP.subtract)
-    act(full("FH"), full("FM"), AF.Copy, scale=0.5)
-    act(full("NEG3"), mat("CRF", ST - 1), AF.Copy, scale=-1.0)
+    fill(full("QTR"), 0.25)
+    scan(full("PW"), full("QTR"), ("ZER", 0, 16), 4.0 ** 16, OP.mult, OP.add)
+    ts(full("PW1"), ("MI", 0, 16), full("PLF"), OP.is_equal)
+    tt(full("PW1"), full("PW1"), full("PW"), OP.mult)
+    add_up(full("WB"), full("PW1"))
+    ts(full("FB"), full("FM"), full("WB"), OP.mult)
+    act(full("FA"), full("FB"), AF.Copy, scale=4.0 ** 16)
+    act(full("FH"), full("FM"), AF.Copy, scale=0.25)
+    act(full("BLB"), full("BLK"), AF.Copy)
+    ts(full("UPR"), full("Z"), full("PL1"), OP.is_ge)
+    copy(full("REPL"), ("MI", 0, 64))
     act(full("IDB"), IDM, AF.Copy)
     ts(full("IDR"), IDM, full("ROWM"), OP.mult)
     ts(full("TRI"), full("Z"), full("PL1"), OP.is_gt)
     fill(full("ALL"), 0.0625)
-    fill(full("ZER"), 0.0)
     fill(full("ONES"), 1.0)
     ts(full("KC"), full("ILF"), -1.0, OP.mult, 31.0, OP.add)
     ts(full("WJ"), full("WI"), 15, OP.bitwise_and)
-    ts(full("WM"), full("WJ"), 0.0, OP.not_equal, 2.0, OP.mult)
-    new_op(P, "V", lambda: g.vector.tensor_tensor_scan(out=ap(("WT", 0, 32)), data0=ap(full("WM")), data1=ap(("ONES", 0, 32)), initial=1.0,
-                                                       op0=OP.mult, op1=OP.max), [full("WM"), ("ONES", 0, 32)], [("WT", 0, 32)], 0.1)
-    act(("WT", 0, 16), ("WT", 16, 32), AF.Copy)
+    ts(("WT", 0, 32), full("WJ"), 0.0, OP.is_equal)
     w = 32
     while w < 2080:
         m = min(w, 2080 - w)
-        act(("WT", w, w + m), ("WT", 0, m), AF.Copy)
+        move(WTQ, ("WT", w, w + m), ("WT", 0, m))
         w += m
     fill(full("BASE"), 0.0)
     fill(full("BASE3"), 0.0)
@@ -464,8 +499,10 @@ def plan(g, core, T, topo):
             ts(sl("BASE", 32 * par + 4 * c0, c, 2 * c), ("ILF", c0, c0 + c), 16.0, OP.mult, 1.0, OP.add)
         ts(sl("BASE", 4 * c0, 2 * c, 3 * c), ("ILF", c0, c0 + c), 9.0, OP.mult)
         ts(sl("BASE3", 2 * c0, 0, c), ("ILF", c0, c0 + c), 16.0, OP.mult, 1.0, OP.add)
-    copy(("LIM", 0, 1), full("TH"))
+    ts(full("TH1"), full("TH"), 1.0, OP.add)
+    ts(("LIM", 0, 1), full("TH"), 1.0, OP.add)
     act(full("NBF"), NB0, AF.Copy)
+    P["late"] = BLATE
     spare = ["b2", "b5", "b6", "b7"]
     for j, lo in enumerate(range(1152, 16 * 1152, 512)):
         hi = min(lo + 512, 16 * 1152)
@@ -473,6 +510,7 @@ def plan(g, core, T, topo):
         cut = [lo] + [x for x in range(1152, 16 * 1152, 1152) if lo < x < hi] + [hi]
         mms(*[((bank, x - lo, y - lo), [(mat("ROT", x // 1152), ("NBF", x % 1152, x % 1152 + y - x))]) for x, y in zip(cut, cut[1:])])
         move(EVAC[j % len(EVAC)], ("NBR", lo, hi), (bank, 0, hi - lo))
+    P["late"] = 0.0
 
     for gen in range(GENS):
         n0 = gen * ST
@@ -484,7 +522,6 @@ def plan(g, core, T, topo):
             n = n0 + t
             end = t == ST - 1
             par = 0 if t == 0 else 1 + (n & 1)
-            places = []
             for b, (l0, w) in enumerate(BATCH):
                 c0, c = l0 // 16, w // 16
                 P["late"] = LATE * b
@@ -495,7 +532,7 @@ def plan(g, core, T, topo):
                 tile = lambda name: (name, l0, l0 + w)
                 ptile = lambda name: (name, 128 * par + l0, 128 * par + l0 + w)
                 wide = lambda name, lo, hi, step=1: sl(name, 16 * l0, lo, hi, step)
-                ghm = ("GHM", 128 * (n & 1) + l0, 128 * (n & 1) + l0 + w)
+                ghm, la, lb = [sl(name, 128 * (n & 1), l0, l0 + w) for name in ("GHM", "LIMA", "LIMB")]
                 if t == 0:
                     l1 = l2 = ("L0", c0, c0 + c)
                     pos, nbw, wtw = ("L0", 8, 8 + c), NB0, ("WT", 0, 32)
@@ -508,8 +545,7 @@ def plan(g, core, T, topo):
                 base = sl("BASE", 32 * par + 4 * c0, 0, 4 * c)
                 if n != ST:
                     gather(ptile("OFF"), nbw, l1)
-                    act(ptile("WW"), wtw, AF.Copy, off=pos)
-                    ts(ptile("M0"), ptile("WW"), 32768.0, OP.is_ge)
+                    pick(M0Q, ptile("M0"), wtw, pos)
                     if not end:
                         act(ptile("HT"), ("IOTA", 0, 1152), AF.Identity, off=l2, bias=1.0)
                         gather2(ptile("DH"), nbw, l1, ptile("HT"), OP.subtract)
@@ -517,35 +553,36 @@ def plan(g, core, T, topo):
                     copy(sl("BASE", 32 * par + 4 * c0, 2 * c, 3 * c), l2)
                 ch = 16 * w // len(GGQ)
                 for j, lo in enumerate(range(0, 16 * w, ch)):
-                    off = sl("OFF", 128 * par + l0, lo // 16, (lo + ch) // 16)
-                    if GGQ[j] == "S":
-                        act(wide("GG", lo, lo + ch), GWIN, AF.Copy, off=off)
-                    else:
-                        gather(wide("GG", lo, lo + ch), GWIN, off)
+                    pick(GGQ[j], wide("GG", lo, lo + ch), GWIN, sl("OFF", 128 * par + l0, lo // 16, (lo + ch) // 16))
                 ep = (bA, 0, w)
-                mms((ep, [(IDM, ("ONES", 0, w))] + sixteen("DIAG", "GG", 16 * l0, 16 * l0 + 16 * w)))
-                copy(tile("EL"), ep)
+                for lo in range(0, w, SUB):
+                    mms(((bA, lo, lo + SUB), [(IDM, ("ONES", 0, SUB))] + sixteen("DIAG", "GG", 16 * (l0 + lo), 16 * (l0 + lo + SUB))))
+                    copy(("EL", l0 + lo, l0 + lo + SUB), (bA, lo, lo + SUB))
                 gather2(ghm, GWIN, l2, ptile("M0"), OP.mult)
                 mms(((bB, 256, 256 + c), [(IDM, ("ONES", 0, c))] + sixteen("CRF", "GHM", ghm[1], ghm[2])))
                 copy(nl, (bB, 256, 256 + c))
                 gather2(tile("DD"), XWIN, nl, a, OP.subtract)
-                for j in range(2):
-                    act(sl("T2", 2 * l0, j, 2 * w, 2), tile("DD"), AF.Abs)
-                for k in range(8):
-                    move(EXPQ[k], wide("TEXP", k, 16 * w, 8), sl("T2", 2 * l0, 0, 2 * w))
+                for lo in range(0, 16 * w, TCH):
+                    act(wide("TEXP", lo, lo + TCH), tile("DD"), AF.Abs, off=("REPL", lo // 16, (lo + TCH) // 16))
+                mms(((bC, 192, 192 + w), [(full("UPR"), ptile("M0"))]))
+                ts(la, (bC, 192, 192 + w), ("LIM", n, n + 1), OP.mult)
+                ts(lb, (bC, 192, 192 + w), 0.0, OP.is_equal, ("LIM", n, n + 1), OP.mult)
                 for lo in range(0, 16 * w, GCH):
                     gather2(wide("UU", lo, lo + GCH), XWIN, sl("EL", l0, lo // 16, (lo + GCH) // 16), wide("TEXP", lo, lo + GCH), OP.add)
-                    act(wide("AB", lo, lo + GCH), wide("UU", lo, lo + GCH), AF.Abs, bias=-255.0)
+                for lo in range(0, 16 * w, ACH):
+                    act(wide("AB", lo, lo + ACH), wide("UU", lo, lo + ACH), AF.Abs, bias=-255.0)
                 mms(((bB, 0, w), sixteen("CRF", "AB", 16 * l0, 16 * l0 + 16 * w)))
-                ts(tile("OK"), (bB, 0, w), ("LIM", n, n + 1), OP.is_le)
-                tt(tile("OKW"), tile("OK"), ptile("WW"), OP.mult)
+                tt(tile("OK"), (bB, 0, w), la, OP.is_lt)
+                tt(tile("OKB"), (bB, 0, w), lb, OP.is_lt)
+                both = [(full("FA"), tile("OK")), (full("FB"), tile("OKB"))]
                 fs, fe, tot = (bB, 64, 64 + w), (bB, 128, 128 + w), (bC, 64, 64 + w)
-                mms((fs, [(full("FM"), tile("OKW"))]), (fe, [(full("FH"), ptile("M0")), (full("FM"), tile("OKW"))]))
-                mms((tot, [(full("BLK"), tile("OKW"))]))
+                mms((fs, both), (fe, [(full("FH"), ptile("M0"))] + both))
+                mms((tot, [(full("BLB"), tile("OK")), (full("BLB"), tile("OKB"))]))
                 act(tile("NF"), tot, AF.Relu, accum=("RF", b, b + 1), scale=-1.0, bias=1.0)
                 pk = lambda j: sl("PACK", 4 * l0, j * w, j * w + w)
                 ts(tile("SEL"), fs, 0.0, OP.is_lt)
                 sa = ("SA", 128 * n + l0, 128 * n + l0 + w)
+                place = sl("POS", 8 * (n & 1), c0, c0 + c)
                 if not end:
                     tt(pk(2), tile("SEL"), ptile("DH"), OP.mult)
                     tt(pk(3), tile("SEL"), ep, OP.mult)
@@ -557,17 +594,18 @@ def plan(g, core, T, topo):
                     for j in range(c):
                         ts(("H", new[1] + j, new[1] + j + 1), (bB, 320 + j, 321 + j), (bB, 320 + 2 * c + j, 321 + 2 * c + j), OP.add)
                     send("rl%d%d" % (n, b), after=["rz%d%d" % (n, h) for h in range(2) if t == 0])
-                    place, idx, pe = lists_at(n, b, o + 1, o + 2), lists_at(n, b, o + 3, o + 4), pk(3)
+                    copy(place, (bB, 320 + c, 320 + 2 * c))
+                    idx, pe = lists_at(n, b, o + 3, o + 4), pk(3)
                 else:
                     tt(pk(1), tile("SEL"), ep, OP.mult)
                     ts(pk(0), fe, 0.0, OP.is_lt, full("PNF"), OP.mult)
                     mms(((bB, 320, 320 + 2 * c), [(IDM, sl("BASE3", 2 * c0, 0, 2 * c))] + sixteen("CRF", "PACK", 4 * l0, 4 * l0 + 2 * w)))
-                    copy(sl("EN", 2 * c0, 0, 2 * c), (bB, 320, 320 + 2 * c))
-                    place, idx, pe = sl("EN", 2 * c0, 0, c), sl("EN", 2 * c0, c, 2 * c), pk(1)
-                tt(tile("NFT"), tile("NF"), sl("T2", 2 * l0, 0, 2 * w, 2), OP.mult)
+                    copy(("EN", c0, c0 + c), (bB, 320 + c, 320 + 2 * c))
+                    copy(place, (bB, 320, 320 + c))
+                    idx, pe = ("EN", c0, c0 + c), pk(1)
+                tt(tile("NFT"), tile("NF"), wide("TEXP", 0, 16 * w, 16), OP.mult)
                 gather2(sa, XWIN, idx, tile("NFT"), OP.add)
                 send("ra%d%d" % (n, b))
-                places.append((place, sa))
                 if end:
                     hl = lambda name, lo, hi: sl(name, 6 * c0, lo * c, hi * c)
                     copy(hl("HF", 0, 6), lists_at(n, b, 5, 11))
@@ -591,19 +629,15 @@ def plan(g, core, T, topo):
             if t < ST - 2:
                 for h in range(2):
                     send("rz%d%d" % (n + 1, h), after=["ra%d%d" % (n, NBAT - 1)])
-            for place, sa in places:
-                scatter(XWIN, place, sa)
+            scatter(XWIN, ("POS", 8 * (n & 1), 8 * (n & 1) + 8), ("SA", 128 * n, 128 * n + 128))
             if n < GENS * ST - 1:
                 mms(((bC, 128, 129), [(full("ALL"), ("RF", b, b + 1)) for b in range(NBAT)]))
                 copy(full("AI"), (bC, 128, 129))
                 ts(full("AI2"), full("AI"), 63, OP.bitwise_and)
-                tt(("LIM", n + 1, n + 2), full("AI2"), full("TH"), OP.add)
-        new_op(P, "V", lambda: g.vector.tensor_reduce(out=ap(full("NRED")), in_=ap(full("IND")), axis=AxisListType.X, op=OP.add),
-               [full("IND")], [full("NRED")], 0.13)
+                ts(("LIM", n + 1, n + 2), full("AI2"), full("TH1"), OP.add)
+        add_up(full("NRED"), full("IND"))
         mms((("b7", 0, 1), [(full("TRI"), full("NRED"))]))
-        new_op(P, "V", lambda: g.vector.tensor_tensor_scan(out=ap(full("PRE")), data0=ap(full("ZER")), data1=ap(full("IND")),
-                                                           initial=ap(("b7", 0, 1)), op0=OP.add, op1=OP.add),
-               [full("IND"), full("ZER"), ("b7", 0, 1)], [full("PRE")], 0.13)
+        scan(full("PRE"), full("ZER"), full("IND"), ("b7", 0, 1), OP.add, OP.add)
         tt(full("PPK"), full("PRE"), full("IND"), OP.mult)
         q1 = ("b7", 16, 24)
         mms((q1, sixteen("CRF", "PPK", 0, 128)))

@@ -7,19 +7,18 @@ AF = ActivationFunctionType
 GENS, ST, N = 2, 4, 8
 BATCH = [(0, 64), (64, 64)]
 NBAT = len(BATCH)
-GCH = 256
-ACH = 256
-TCH = 256
-SUB = 64
+TCUT = (256, 256, 256, 256)
+UCUT = (256, 256, 256, 128, 128)
+ACUT = (256, 256, 256, 128, 128)
+SUB = 32
 GGQ = "SVSS"
-M0Q = "S"
-WTQ = "V"
-EVAC = "SVSSV"
-LOADS = (3.5, 1.5, 1.5, 0.1)
-FARUS = 3.7
-LATE = 5.0
+NBQ = "SV"
+EVAC = "SV"
+LOADS = (4.0, 2.3, 2.2)
+FARUS = 3.2
+LATES = (3.5, 4.0, 4.5, 5.0, 5.5, 6.0)
 BLATE = 0.0
-WAKE = 0.23
+WAKE = 0.24
 PASSES = 6
 CPE = 0.00043
 HS = 48
@@ -27,26 +26,25 @@ HS = 48
 F32, F16, BF, I32, U16 = "float32", "float16", "bfloat16", "int32", "uint16"
 SB = {
     "GW": (1152, I32), "NBR": (16 * 1152, I32), "NBF": (1152, F16), "XT": (2064, BF), "A0": (128, BF), "TH": (1, I32),
-    "PI": (1, I32), "PS": (1, I32), "PL": (1, I32), "PSF": (1, F32), "PLF": (1, F32), "PL1": (1, F32), "PNF": (1, F32), "C1S": (1, F32),
+    "PI": (1, I32), "PS": (1, I32), "PL": (1, I32), "PSF": (1, F32), "PLF": (1, F32), "PL1": (1, F32), "C1S": (1, F32),
     "PLM": (1, F32), "ROWM": (1, F32), "WB": (1, F32), "TH1": (1, F32), "C16": (8, I32), "ILF": (8, F32), "KC": (8, F32),
     "MI": (128, I32), "MS": (128, I32), "ML": (128, I32), "ML1": (128, F16), "RI": (128, I32), "RJ": (128, I32), "RK": (128, F16),
     "BLK": (128, F16), "BLB": (128, BF), "Z": (128, F16), "ZD": (128, F16), "ZR": (128, F16), "ID": (128, F16), "ID2": (128, F16),
     "IDB": (128, BF), "IDR": (128, F16), "CRF": (2048, F16), "DIAG": (2048, F16), "ROT": (2048, F16), "FM": (128, F16), "FA": (128, BF),
     "FB": (128, BF), "FH": (128, BF), "UPR": (128, BF), "NEG3": (128, F16), "TRI": (128, F32), "ALL": (128, F32), "ZER": (128, F16),
-    "ONES": (128, F16), "QTR": (16, F32), "PW": (16, F32), "PW1": (16, F32), "WI": (32, I32), "WJ": (32, I32), "WT": (2080, BF),
-    "IOTA": (2064, I32), "L0": (16, U16), "REPL": (64, U16), "BASE3": (16, F16),
-    "OFF": (3 * 128, U16), "M0": (3 * 128, BF), "HT": (3 * 128, F16), "DH": (3 * 128, F16), "BASE": (3 * 32, F16), "GHM": (2 * 128, F16),
+    "ONES": (128, F16), "QTR": (16, F32), "PW": (16, F32), "PW1": (16, F32), "FR": (128, F16), "GA": (128, BF), "GB": (128, BF),
+    "M0": (128, BF), "IOTA": (2064, I32), "L0": (8, U16), "REPL": (64, U16), "BASE3": (16, F16),
+    "OFF": (3 * 128, U16), "HT": (3 * 128, F16), "DH": (3 * 128, F16), "BASE": (3 * 32, F16), "GHM": (2 * 128, F16),
     "LIMA": (256, F32), "LIMB": (256, F32), "POS": (16, U16),
     "DD": (128, BF), "TEXP": (2048, BF), "GG": (2048, F16), "EL": (128, U16), "UU": (2048, F16), "AB": (2048, F16), "OK": (128, BF),
     "OKB": (128, BF), "SEL": (128, F16), "PACK": (512, F16), "NF": (128, F16), "NFT": (128, BF), "EN": (8, U16),
     "RF": (NBAT, F32), "AI": (1, I32), "AI2": (1, I32), "LIM": (8, F32),
     "HF": (48, F32), "HZ": (48, F32), "HM": (48, F32), "HV": (48, F32), "VL": (48, U16),
     "E1": (8, F32), "E2": (8, F32), "EU": (8, U16), "CM": (128, F16), "VT": (3 * 128, F16), "GHF": (128, F16), "DT": (128, F16),
-    "IND": (128, F16), "NRED": (1, F32), "PRE": (128, F32), "PPK": (128, F16), "POSL": (8, U16), "SD": (128, F32),
-    "GEC": (8, F32), "DQ": (8, F32), "MLQ": (8, F32), "IDN": (8, U16), "OW": (160, F32), "NEW": (128, F32), "YA": (128, F32),
-    "YS": (128, F32),
+    "IND": (128, F16), "NRED": (1, F32), "PRE": (128, F32), "PPK": (128, F16), "POSL": (8, U16),
+    "GEC": (8, F32), "DQ": (8, F32), "MLQ": (8, F32), "IDN": (8, U16), "NEW": (128, F32), "YA": (128, F32), "YS": (128, F32),
     "H": (GENS * ST * NBAT * HS, U16), "SA": (GENS * ST * 128, BF), "LA": (GENS * ST * 128, BF), "DZ": (GENS * ST * 128, F16),
-    "SM": (GENS * 24, F16), "LM": (GENS * 24, F16), "SO": (GENS * 16, F16), "LO": (GENS * 16, F16),
+    "SP": (GENS * ST * 128, BF), "LP": (GENS * ST * 128, BF), "SD": (GENS * 136, F32), "OW": (GENS * 168, F32), "LO": (GENS * 32, F32),
 }
 SCRATCH = {}
 POOLED = {}
@@ -76,15 +74,16 @@ def messages():
             for b, (l0, w) in enumerate(BATCH):
                 if t < ST - 1:
                     o = 2 * (ST - 1 - t)
-                    out["rl%d%d" % (n, b)] = (1, lists_at(n, b, o, 11), lists_at(n + 1, b, o, 11), b % 2)
+                    out["rl%d%d" % (n, b)] = (1, lists_at(n, b, o + 1, 11), lists_at(n + 1, b, o + 1, 11), b % 2)
+                    out["rp%d%d" % (n, b)] = (1, ("SP", 128 * n + l0, 128 * n + l0 + w), ("LP", 128 * n + l0, 128 * n + l0 + w), b % 2)
                 out["ra%d%d" % (n, b)] = (1 if t < ST - 1 else N - ST + 1, ("SA", 128 * n + l0, 128 * n + l0 + w),
                                           ("LA", 128 * n + l0, 128 * n + l0 + w), b % 2)
             if t < ST - 1:
                 for h in range(2):
                     out["rz%d%d" % (n, h)] = (1, ("DZ", 128 * n + 64 * h, 128 * n + 64 * h + 64),
                                               ("DZ", 128 * n + 128 + 64 * h, 128 * n + 192 + 64 * h), h)
-        out["rm%d" % g] = (N - ST + 1, ("SM", 24 * g, 24 * g + 24), ("LM", 24 * g, 24 * g + 24), 0)
-        out["ro%d" % g] = (N - ST + 2, ("SO", 16 * g, 16 * g + 16), ("LO", 16 * g, 16 * g + 16), 1)
+        out["rm%d" % g] = (N - ST + 1, ("SD", 136 * g + 96, 136 * g + 136), ("OW", 168 * g + 128, 168 * g + 168), 0)
+        out["ro%d" % g] = (N - ST + 2, ("SD", 136 * g + 96, 136 * g + 128), ("LO", 32 * g, 32 * g + 32), 1)
     return out
 
 
@@ -208,9 +207,10 @@ def order_ops(ops):
     way = [0.0] * n
     for k in range(n - 1, -1, -1):
         way[k] = ops[k]["dur"] + ops[k]["lat"] + WAKE + max([way[s] for s in succ[k]] or [0.0])
-    key = [(ops[k]["late"] - way[k], k) for k in range(n)]
     best = None
-    for _i in range(PASSES):
+    for i in range(PASSES * len(LATES)):
+        if i % PASSES == 0:
+            key = [(ops[k]["late"] * LATES[i // PASSES] - way[k], k) for k in range(n)]
         lo, hi = place_ops(ops, pred, succ, key, False)
         total = max(hi[k] + ops[k]["lat"] for k in range(n))
         if best is None or total < best[0]:
@@ -417,21 +417,24 @@ def plan(g, core, T, topo):
     def full(name):
         return (name, 0, SB[name][0])
 
+    def pieces(sizes):
+        return [(sum(sizes[:j]), sum(sizes[:j + 1])) for j in range(len(sizes))]
+
     def sixteen(name, buf, lo, hi):
         return [(mat(name, r), (buf, lo + r, hi, 16)) for r in range(16)]
 
     GWIN, XWIN, NB0, IDM = full("GW"), ("XT", 0, 2049), ("NBR", 0, 1152), full("ID")
 
-    load("S", full("TH"), "th", "dm3", 0.0)
+    load("S", full("TH"), "th", "dm3", 2.5)
+    load("S", full("A0"), "a0", "dm2", 0.5)
+    loads.clear()
     load("Y", NB0, "nb", "dm0", LOADS[0])
     load("Y", GWIN, "gn", "dm1", LOADS[1])
     load("Y", ("XT", 1, 2049), "x", "dm4", LOADS[2], [("XT", 0, 1)])
-    load("Y", full("A0"), "a0", "dm2", LOADS[3])
     fill(("XT", 0, 1), 0.0)
     iota(full("PI"), [[1, 1]], 0, 1)
     iota(full("MI"), [[1, 128]], 0, 0)
     iota(full("C16"), [[16, 8]], 0, 0)
-    iota(full("WI"), [[1, 32]], 127, -1)
     iota(full("RI"), [[1, 128]], 128, -1)
     iota(("IOTA", 0, 1152), [[1, 1152]], -1, 0)
     iota(("IOTA", 1152, 2064), [[1, 912]], 1151, 0)
@@ -440,13 +443,11 @@ def plan(g, core, T, topo):
     copy(full("PSF"), full("PS"))
     copy(full("PLF"), full("PL"))
     ts(full("PL1"), full("PL"), 1.0, OP.add)
-    ts(full("PNF"), full("PL1"), 16.0, OP.is_lt, full("PL1"), OP.mult)
     ts(full("PLM"), full("PL"), -1.0, OP.add)
-    ts(full("C1S"), full("PNF"), 1152.0, OP.mult)
+    ts(full("C1S"), full("PL"), 1152.0, OP.mult)
     ts(full("ROWM"), full("PL"), 4.0, OP.is_ge)
     ts(full("ILF"), full("C16"), full("PLF"), OP.add)
-    ts(("L0", 0, 8), full("ILF"), 9.0, OP.mult)
-    fill(("L0", 8, 16), 1)
+    ts(full("L0"), full("ILF"), 9.0, OP.mult)
     ts(full("MS"), full("MI"), 4, OP.arith_shift_right)
     ts(full("ML"), full("MI"), 15, OP.bitwise_and)
     ts(full("ML1"), full("ML"), 1.0, OP.add)
@@ -474,7 +475,12 @@ def plan(g, core, T, topo):
     add_up(full("WB"), full("PW1"))
     ts(full("FB"), full("FM"), full("WB"), OP.mult)
     act(full("FA"), full("FB"), AF.Copy, scale=4.0 ** 16)
-    act(full("FH"), full("FM"), AF.Copy, scale=0.25)
+    ts(full("FR"), mat("ROT", 1), -2.0, OP.mult)
+    tt(full("FR"), full("FR"), full("BLK"), OP.add)
+    ts(full("GB"), full("FR"), full("WB"), OP.mult)
+    act(full("GA"), full("GB"), AF.Copy, scale=4.0 ** 16)
+    act(full("FH"), full("FR"), AF.Copy, scale=0.25)
+    ts(full("M0"), full("ZER"), full("PLF"), OP.is_equal)
     act(full("BLB"), full("BLK"), AF.Copy)
     ts(full("UPR"), full("Z"), full("PL1"), OP.is_ge)
     copy(full("REPL"), ("MI", 0, 64))
@@ -484,13 +490,6 @@ def plan(g, core, T, topo):
     fill(full("ALL"), 0.0625)
     fill(full("ONES"), 1.0)
     ts(full("KC"), full("ILF"), -1.0, OP.mult, 31.0, OP.add)
-    ts(full("WJ"), full("WI"), 15, OP.bitwise_and)
-    ts(("WT", 0, 32), full("WJ"), 0.0, OP.is_equal)
-    w = 32
-    while w < 2080:
-        m = min(w, 2080 - w)
-        move(WTQ, ("WT", w, w + m), ("WT", 0, m))
-        w += m
     fill(full("BASE"), 0.0)
     fill(full("BASE3"), 0.0)
     for b, (l0, w) in enumerate(BATCH):
@@ -501,7 +500,9 @@ def plan(g, core, T, topo):
         ts(sl("BASE3", 2 * c0, 0, c), ("ILF", c0, c0 + c), 16.0, OP.mult, 1.0, OP.add)
     ts(full("TH1"), full("TH"), 1.0, OP.add)
     ts(("LIM", 0, 1), full("TH"), 1.0, OP.add)
-    act(full("NBF"), NB0, AF.Copy)
+    for j, q in enumerate(NBQ):
+        m = 1152 // len(NBQ)
+        move(q, ("NBF", m * j, m * j + m), ("NBR", m * j, m * j + m))
     P["late"] = BLATE
     spare = ["b2", "b5", "b6", "b7"]
     for j, lo in enumerate(range(1152, 16 * 1152, 512)):
@@ -515,7 +516,7 @@ def plan(g, core, T, topo):
     for gen in range(GENS):
         n0 = gen * ST
         act(("DZ", 128 * n0, 128 * n0 + 128), ("GW", 0, 1152, 9), AF.Copy)
-        act(("OW", 0, 128), ("GW", 0, 1152, 9), AF.Copy)
+        act(sl("OW", 168 * gen, 0, 128), ("GW", 0, 1152, 9), AF.Copy)
         for h in range(2):
             send("rz%d%d" % (n0, h), lat=6.0 if gen == 0 else 0.0)
         for t in range(ST):
@@ -524,7 +525,7 @@ def plan(g, core, T, topo):
             par = 0 if t == 0 else 1 + (n & 1)
             for b, (l0, w) in enumerate(BATCH):
                 c0, c = l0 // 16, w // 16
-                P["late"] = LATE * b
+                P["late"] = b
                 bA, bB, bC = ["b%d" % (3 * (b % 2) + i) for i in range(3)]
                 if n == 0:
                     bC = bA
@@ -535,17 +536,16 @@ def plan(g, core, T, topo):
                 ghm, la, lb = [sl(name, 128 * (n & 1), l0, l0 + w) for name in ("GHM", "LIMA", "LIMB")]
                 if t == 0:
                     l1 = l2 = ("L0", c0, c0 + c)
-                    pos, nbw, wtw = ("L0", 8, 8 + c), NB0, ("WT", 0, 32)
+                    nbw, m0 = NB0, tile("M0")
                     a = tile("A0") if gen == 0 else ("LA", 128 * (n - 1) + l0, 128 * (n - 1) + l0 + w)
                 else:
-                    l1, pos, l2 = lists_at(n, b, o + 2, o + 3), lists_at(n, b, o + 3, o + 4), lists_at(n, b, o + 4, o + 5)
-                    nbw, wtw = full("NBR"), ("WT", 0, 2064)
+                    l1, l2 = lists_at(n, b, o + 3, o + 4), lists_at(n, b, o + 4, o + 5)
+                    nbw, m0 = full("NBR"), ("LP", 128 * (n - 1) + l0, 128 * (n - 1) + l0 + w)
                     a = ("LA", 128 * (n - 1) + l0, 128 * (n - 1) + l0 + w)
                 nl = lists_at(n, b, o + 4, o + 5)
                 base = sl("BASE", 32 * par + 4 * c0, 0, 4 * c)
                 if n != ST:
                     gather(ptile("OFF"), nbw, l1)
-                    pick(M0Q, ptile("M0"), wtw, pos)
                     if not end:
                         act(ptile("HT"), ("IOTA", 0, 1152), AF.Identity, off=l2, bias=1.0)
                         gather2(ptile("DH"), nbw, l1, ptile("HT"), OP.subtract)
@@ -554,29 +554,29 @@ def plan(g, core, T, topo):
                 ch = 16 * w // len(GGQ)
                 for j, lo in enumerate(range(0, 16 * w, ch)):
                     pick(GGQ[j], wide("GG", lo, lo + ch), GWIN, sl("OFF", 128 * par + l0, lo // 16, (lo + ch) // 16))
-                ep = (bA, 0, w)
-                for lo in range(0, w, SUB):
-                    mms(((bA, lo, lo + SUB), [(IDM, ("ONES", 0, SUB))] + sixteen("DIAG", "GG", 16 * (l0 + lo), 16 * (l0 + lo + SUB))))
-                    copy(("EL", l0 + lo, l0 + lo + SUB), (bA, lo, lo + SUB))
-                gather2(ghm, GWIN, l2, ptile("M0"), OP.mult)
+                eps = [(lo, (bA if lo == 0 or n == 0 else "b%d" % (6 + b), lo, lo + SUB)) for lo in range(0, w, SUB)]
+                for lo, ep in eps:
+                    mms((ep, [(IDM, ("ONES", 0, SUB))] + sixteen("DIAG", "GG", 16 * (l0 + lo), 16 * (l0 + lo + SUB))))
+                    copy(("EL", l0 + lo, l0 + lo + SUB), ep)
+                gather2(ghm, GWIN, l2, m0, OP.mult)
                 mms(((bB, 256, 256 + c), [(IDM, ("ONES", 0, c))] + sixteen("CRF", "GHM", ghm[1], ghm[2])))
                 copy(nl, (bB, 256, 256 + c))
                 gather2(tile("DD"), XWIN, nl, a, OP.subtract)
-                for lo in range(0, 16 * w, TCH):
-                    act(wide("TEXP", lo, lo + TCH), tile("DD"), AF.Abs, off=("REPL", lo // 16, (lo + TCH) // 16))
-                mms(((bC, 192, 192 + w), [(full("UPR"), ptile("M0"))]))
+                for lo, hi in pieces(TCUT):
+                    act(wide("TEXP", lo, hi), tile("DD"), AF.Abs, off=("REPL", lo // 16, hi // 16))
+                mms(((bC, 192, 192 + w), [(full("UPR"), m0)]))
                 ts(la, (bC, 192, 192 + w), ("LIM", n, n + 1), OP.mult)
                 ts(lb, (bC, 192, 192 + w), 0.0, OP.is_equal, ("LIM", n, n + 1), OP.mult)
-                for lo in range(0, 16 * w, GCH):
-                    gather2(wide("UU", lo, lo + GCH), XWIN, sl("EL", l0, lo // 16, (lo + GCH) // 16), wide("TEXP", lo, lo + GCH), OP.add)
-                for lo in range(0, 16 * w, ACH):
-                    act(wide("AB", lo, lo + ACH), wide("UU", lo, lo + ACH), AF.Abs, bias=-255.0)
+                for lo, hi in pieces(UCUT):
+                    gather2(wide("UU", lo, hi), XWIN, sl("EL", l0, lo // 16, hi // 16), wide("TEXP", lo, hi), OP.add)
+                for lo, hi in pieces(ACUT):
+                    act(wide("AB", lo, hi), wide("UU", lo, hi), AF.Abs, bias=-255.0)
                 mms(((bB, 0, w), sixteen("CRF", "AB", 16 * l0, 16 * l0 + 16 * w)))
                 tt(tile("OK"), (bB, 0, w), la, OP.is_lt)
                 tt(tile("OKB"), (bB, 0, w), lb, OP.is_lt)
                 both = [(full("FA"), tile("OK")), (full("FB"), tile("OKB"))]
                 fs, fe, tot = (bB, 64, 64 + w), (bB, 128, 128 + w), (bC, 64, 64 + w)
-                mms((fs, both), (fe, [(full("FH"), ptile("M0"))] + both))
+                mms((fs, both), (fe, [(full("FH"), m0), (full("GA"), tile("OK")), (full("GB"), tile("OKB"))]))
                 mms((tot, [(full("BLB"), tile("OK")), (full("BLB"), tile("OKB"))]))
                 act(tile("NF"), tot, AF.Relu, accum=("RF", b, b + 1), scale=-1.0, bias=1.0)
                 pk = lambda j: sl("PACK", 4 * l0, j * w, j * w + w)
@@ -585,20 +585,24 @@ def plan(g, core, T, topo):
                 place = sl("POS", 8 * (n & 1), c0, c0 + c)
                 if not end:
                     tt(pk(2), tile("SEL"), ptile("DH"), OP.mult)
-                    tt(pk(3), tile("SEL"), ep, OP.mult)
+                    for lo, ep in eps:
+                        tt(sl("PACK", 4 * l0 + 3 * w, lo, lo + SUB), sl("SEL", l0, lo, lo + SUB), ep, OP.mult)
                     ts(pk(0), fe, 0.0, OP.is_lt, full("C1S"), OP.mult)
-                    ts(pk(1), fe, 0.0, OP.is_lt, full("PNF"), OP.mult)
+                    ts(pk(1), fe, 0.0, OP.is_lt, full("PLF"), OP.mult)
+                    ts(("SP", 128 * n + l0, 128 * n + l0 + w), fe, 0.0, OP.is_lt)
+                    send("rp%d%d" % (n, b), after=["rz%d%d" % (n, h) for h in range(2) if t == 0])
                     mms(((bB, 320, 320 + 4 * c), [(IDM, base)] + sixteen("CRF", "PACK", 4 * l0, 4 * l0 + 4 * w)))
-                    copy(lists_at(n, b, o + 1, o + 4), (bB, 320 + c, 320 + 4 * c))
-                    new = lists_at(n, b, o, o + 1)
+                    copy(lists_at(n, b, o + 2, o + 4), (bB, 320 + 2 * c, 320 + 4 * c))
+                    new = lists_at(n, b, o + 1, o + 2)
                     for j in range(c):
                         ts(("H", new[1] + j, new[1] + j + 1), (bB, 320 + j, 321 + j), (bB, 320 + 2 * c + j, 321 + 2 * c + j), OP.add)
-                    send("rl%d%d" % (n, b), after=["rz%d%d" % (n, h) for h in range(2) if t == 0])
+                    send("rl%d%d" % (n, b), after=["rp%d%d" % (n, b)])
                     copy(place, (bB, 320 + c, 320 + 2 * c))
                     idx, pe = lists_at(n, b, o + 3, o + 4), pk(3)
                 else:
-                    tt(pk(1), tile("SEL"), ep, OP.mult)
-                    ts(pk(0), fe, 0.0, OP.is_lt, full("PNF"), OP.mult)
+                    for lo, ep in eps:
+                        tt(sl("PACK", 4 * l0 + w, lo, lo + SUB), sl("SEL", l0, lo, lo + SUB), ep, OP.mult)
+                    ts(pk(0), fe, 0.0, OP.is_lt, full("PLF"), OP.mult)
                     mms(((bB, 320, 320 + 2 * c), [(IDM, sl("BASE3", 2 * c0, 0, 2 * c))] + sixteen("CRF", "PACK", 4 * l0, 4 * l0 + 2 * w)))
                     copy(("EN", c0, c0 + c), (bB, 320 + c, 320 + 2 * c))
                     copy(place, (bB, 320, 320 + c))
@@ -621,10 +625,10 @@ def plan(g, core, T, topo):
                         act(sl("VT", 128 * j, l0, l0 + w), ("IOTA", 0, 2049), AF.Copy, off=hl("VL", 4 - 2 * j, 5 - 2 * j))
                     tt(tile("IND"), tile("NF"), tile("CM"), OP.is_equal)
                     tt(tile("GHF"), tile("NF"), ghm, OP.mult)
-                    mms((("b6", l0, l0 + w), [(full("IDR"), ("DZ", 128 * n + l0, 128 * n + l0 + w))]
+                    mms(((bC, 256, 256 + w), [(full("IDR"), ("DZ", 128 * n + l0, 128 * n + l0 + w))]
                          + [(mat("DIAG", j), sl("VT", 128 * j, l0, l0 + w)) for j in range(ST - 1)]
                          + [(mat("CRF", t), pe), (mat("CRF", t), tile("GHF")), (full("NEG3"), tile("SEL"))]))
-                    act(tile("DT"), ("b6", l0, l0 + w), AF.Copy)
+                    act(tile("DT"), (bC, 256, 256 + w), AF.Copy)
             P["late"] = 0.0
             if t < ST - 2:
                 for h in range(2):
@@ -642,19 +646,16 @@ def plan(g, core, T, topo):
         q1 = ("b7", 16, 24)
         mms((q1, sixteen("CRF", "PPK", 0, 128)))
         ts(full("POSL"), q1, -1.0, OP.mult, 128.0, OP.add)
-        scatter(full("SD"), full("POSL"), full("DT"))
-        copy(("SM", 24 * gen + 8, 24 * gen + 24), ("SD", 97, 128, 2))
-        act(("SO", 16 * gen, 16 * gen + 16), ("SD", 96, 128, 2), AF.Copy)
+        scatter(sl("SD", 136 * gen, 0, 128), full("POSL"), full("DT"))
         ts(full("GEC"), q1, 97.0, OP.is_ge)
         tt(full("DQ"), full("KC"), q1, OP.add)
         tt(full("MLQ"), full("GEC"), full("DQ"), OP.mult)
-        tt(("SM", 24 * gen, 24 * gen + 8), full("MLQ"), full("ILF"), OP.add)
+        tt(sl("SD", 136 * gen, 128, 136), full("MLQ"), full("ILF"), OP.add)
         send("ro%d" % gen)
         send("rm%d" % gen)
-        copy(full("IDN"), ("LM", 24 * gen, 24 * gen + 8))
-        act(("OW", 129, 160, 2), ("LM", 24 * gen + 8, 24 * gen + 24), AF.Copy)
-        act(("OW", 128, 160, 2), ("LO", 16 * gen, 16 * gen + 16), AF.Copy)
-        gather(("GW", 0, 1152, 9) if gen < GENS - 1 else full("NEW"), full("OW"), full("IDN"))
+        copy(full("IDN"), sl("OW", 168 * gen, 160, 168))
+        act(sl("OW", 168 * gen, 128, 160, 2), sl("LO", 32 * gen, 0, 32, 2), AF.Copy)
+        gather(("GW", 0, 1152, 9) if gen < GENS - 1 else full("NEW"), sl("OW", 168 * gen, 0, 160), full("IDN"))
     store("yg", full("NEW"), "dm5")
     act(full("YA"), ("LA", 128 * (GENS * ST - 1), 128 * GENS * ST), AF.Copy)
     store("ya", full("YA"), "dm6")

import numpy as np
from concourse.bass import DstId, RemoteDMATransfer
from concourse.mybir import dt, AluOpType, AxisListType, ActivationFunctionType

OP = AluOpType
AF = ActivationFunctionType
GENS, ST, N = 2, 4, 8
BATCH = [(0, 64), (64, 64)]
NBAT = len(BATCH)
TCUT = (256, 256, 256, 256)
UCUT = (256, 256, 256, 128, 128)
ACUT = (256, 256, 256, 128, 128)
SUB = 32
GGQ = "SVSS"
NBQ = "SV"
EVAC = "SV"
LOADS = (4.0, 2.3, 2.2)
FARUS = 3.2
LATES = (3.5, 4.0, 4.5, 5.0, 5.5, 6.0)
BLATE = 0.0
WAKE = 0.24
PASSES = 6
CPE = 0.00043
HS = 48

F32, F16, BF, I32, U16 = "float32", "float16", "bfloat16", "int32", "uint16"
SB = {
    "GW": (1152, I32), "NBR": (16 * 1152, I32), "NBF": (1152, F16), "XT": (2064, BF), "A0": (128, BF), "TH": (1, I32),
    "PI": (1, I32), "PS": (1, I32), "PL": (1, I32), "PSF": (1, F32), "PLF": (1, F32), "PL1": (1, F32), "C1S": (1, F32),
    "PLM": (1, F32), "ROWM": (1, F32), "WB": (1, F32), "TH1": (1, F32), "C16": (8, I32), "ILF": (8, F32), "KC": (8, F32),
    "MI": (128, I32), "MS": (128, I32), "ML": (128, I32), "ML1": (128, F16), "RI": (128, I32), "RJ": (128, I32), "RK": (128, F16),
    "BLK": (128, F16), "BLB": (128, BF), "Z": (128, F16), "ZD": (128, F16), "ZR": (128, F16), "ID": (128, F16), "ID2": (128, F16),
    "IDB": (128, BF), "IDR": (128, F16), "CRF": (2048, F16), "DIAG": (2048, F16), "ROT": (2048, F16), "FM": (128, F16), "FA": (128, BF),
    "FB": (128, BF), "FH": (128, BF), "UPR": (128, BF), "NEG3": (128, F16), "TRI": (128, F32), "ALL": (128, F32), "ZER": (128, F16),
    "ONES": (128, F16), "QTR": (16, F32), "PW": (16, F32), "PW1": (16, F32), "FR": (128, F16), "GA": (128, BF), "GB": (128, BF),
    "M0": (128, BF), "IOTA": (2064, I32), "L0": (8, U16), "REPL": (64, U16), "BASE3": (16, F16),
    "OFF": (3 * 128, U16), "HT": (3 * 128, F16), "DH": (3 * 128, F16), "BASE": (3 * 32, F16), "GHM": (2 * 128, F16),
    "LIMA": (256, F32), "LIMB": (256, F32), "POS": (16, U16),
    "DD": (128, BF), "TEXP": (2048, BF), "GG": (2048, F16), "EL": (128, U16), "UU": (2048, F16), "AB": (2048, F16), "OK": (128, BF),
    "OKB": (128, BF), "SEL": (128, F16), "PACK": (512, F16), "NF": (128, F16), "NFT": (128, BF), "EN": (8, U16),
    "RF": (NBAT, F32), "AI": (1, I32), "AI2": (1, I32), "LIM": (8, F32),
    "HF": (48, F32), "HZ": (48, F32), "HM": (48, F32), "HV": (48, F32), "VL": (48, U16),
    "E1": (8, F32), "E2": (8, F32), "EU": (8, U16), "CM": (128, F16), "VT": (3 * 128, F16), "GHF": (128, F16), "DT": (128, F16),
    "IND": (128, F16), "NRED": (1, F32), "PRE": (128, F32), "PPK": (128, F16), "POSL": (8, U16),
    "GEC": (8, F32), "DQ": (8, F32), "MLQ": (8, F32), "IDN": (8, U16), "NEW": (128, F32), "YA": (128, F32), "YS": (128, F32),
    "H": (GENS * ST * NBAT * HS, U16), "SA": (GENS * ST * 128, BF), "LA": (GENS * ST * 128, BF), "DZ": (GENS * ST * 128, F16),
    "SP": (GENS * ST * 128, BF), "LP": (GENS * ST * 128, BF), "SD": (GENS * 136, F32), "OW": (GENS * 168, F32), "LO": (GENS * 32, F32),
}
SCRATCH = {}
POOLED = {}
for _n in SB:
    if SB[_n][0] <= 8 and SB[_n][1] in (F32, I32) and _n != "TH":
        _b = "K" + SB[_n][1]
        _at = SCRATCH[_b][1][1] if _b in SCRATCH else 0
        POOLED[_n] = (_b, _at)
        SCRATCH[_b] = ("sbuf", [128, _at + SB[_n][0]], SB[_n][1])
    else:
        SCRATCH[_n] = ("sbuf", [128, SB[_n][0]], SB[_n][1])
for _i in range(8):
    SCRATCH["b%d" % _i] = ("psum", [128, 512], F32)


def lists_at(n, b, lo, hi):
    c = BATCH[b][1] // 16
    at = (n * NBAT + b) * HS
    return ("H", at + lo * c, at + hi * c)


def messages():
    out = {}
    for g in range(GENS):
        for t in range(ST):
            n = g * ST + t
            for b, (l0, w) in enumerate(BATCH):
                if t < ST - 1:
                    o = 2 * (ST - 1 - t)
                    out["rl%d%d" % (n, b)] = (1, lists_at(n, b, o + 1, 11), lists_at(n + 1, b, o + 1, 11), b % 2)
                    out["rp%d%d" % (n, b)] = (1, ("SP", 128 * n + l0, 128 * n + l0 + w), ("LP", 128 * n + l0, 128 * n + l0 + w), b % 2)
                out["ra%d%d" % (n, b)] = (1 if t < ST - 1 else N - ST + 1, ("SA", 128 * n + l0, 128 * n + l0 + w),
                                          ("LA", 128 * n + l0, 128 * n + l0 + w), b % 2)
            if t < ST - 1:
                for h in range(2):
                    out["rz%d%d" % (n, h)] = (1, ("DZ", 128 * n + 64 * h, 128 * n + 64 * h + 64),
                                              ("DZ", 128 * n + 128 + 64 * h, 128 * n + 192 + 64 * h), h)
        out["rm%d" % g] = (N - ST + 1, ("SD", 136 * g + 96, 136 * g + 136), ("OW", 168 * g + 128, 168 * g + 168), 0)
        out["ro%d" % g] = (N - ST + 2, ("SD", 136 * g + 96, 136 * g + 128), ("LO", 32 * g, 32 * g + 32), 1)
    return out


MSG = messages()
NPOOL = 150 - len(MSG) - 9
SEMAPHORES = list(MSG) + ["ls"] + ["dm%d" % i for i in range(8)] + ["p%d" % i for i in range(NPOOL)]


def route(src, dst, topo, pick):
    if topo.may_write(src, dst):
        return [src, dst]
    c = [x for x in topo.cores_of(src) if x != src and topo.may_write(x, dst)]
    c.sort(key=lambda x: (topo.die(x) != topo.die(src), x))
    return [src, c[pick % len(c)], dst]


def hop(g, T, topo, a, b, src, land, sem):
    rid, pid = topo.addr(b, a)
    g.remote_dma(T[land[0]][:, land[1]:land[2]], T[src[0]][:, src[1]:src[2]], T.sem[sem], T.sem["ls"], pid, rid, topo.mask(a, b))
    return len(topo.engines(a, b))


def relay_program(g, core, T, topo):
    total = 0
    for c in [x for x in T.cores if x in topo.cores_of(core)]:
        r = T.rank_of(c)
        if "sends" not in order_cache:
            ops, seq, _s = plan(g, c, T, topo)
            order_cache["sends"] = [ops[k]["msg"] for k in seq if ops[k]["msg"]]
        for sem in order_cache["sends"]:
            on, src, land, pick = MSG[sem]
            way = route(c, T.cores[(r + on) % N], topo, pick)
            if len(way) == 3 and way[1] == core:
                g.wait_ge(T.sem[sem], len(topo.engines(c, core)))
                total += hop(g, T, topo, core, way[2], land, land, sem)
    if total:
        g.wait_ge(T.sem["ls"], total)


def bits(lo, hi, step):
    if step == 1:
        return ((1 << (hi - lo)) - 1) << lo
    m = 0
    for i in range(lo, hi, step):
        m |= 1 << i
    return m


span_cache = {}
order_cache = {}


def new_op(P, q, emit, rd, wr, dur, sem=None, amount=1, sdeps=(), lat=0.0, msg=None):
    ops, track, banks = P["ops"], P["track"], P["banks"]
    k = len(ops)
    deps = set()
    for acc, isw in [(a, False) for a in rd] + [(a, True) for a in wr]:
        name = acc[0]
        key = (acc[1], acc[2], acc[3] if len(acc) > 3 else 1)
        if key not in span_cache:
            span_cache[key] = bits(*key)
        m = span_cache[key]
        Wr, R = track.setdefault(name, ([], []))
        for mm, o in Wr:
            if mm & m and o != k:
                deps.add(o)
        if isw:
            for mm, o in R:
                if mm & m and o != k:
                    deps.add(o)
            Wr[:] = [(mm & ~m, o) for mm, o in Wr if mm & ~m] + [(m, k)]
            R[:] = [(mm & ~m, o) for mm, o in R if mm & ~m]
        else:
            R.append((m, k))
        if name in banks:
            for o in banks[name]:
                if o != k and ops[o]["q"] != q:
                    deps.add(o)
            banks[name][:] = [o for o in banks[name] if o != k and ops[o]["q"] == q]
            banks[name].append(k)
    ops.append({"q": q, "emit": emit, "deps": deps, "sdeps": set(sdeps), "dur": dur, "sem": sem, "amount": amount, "lat": lat, "msg": msg,
                "late": P["late"]})
    return k


def place_ops(ops, before, after, key, back):
    n = len(ops)
    left = [len(before[k]) for k in range(n)]
    ready, lo_of, hi_of, busy = [0.0] * n, [0.0] * n, [0.0] * n, {}
    cand = [k for k in range(n) if left[k] == 0]
    while cand:
        k = min(cand, key=lambda x: key[x])
        cand.remove(k)
        o = ops[k]
        s, dur = ready[k] + (o["lat"] if back else 0.0), o["dur"]
        if o["q"] != "recv":
            taken = busy.setdefault(o["q"], [])
            at = len(taken)
            while at > 0 and taken[at - 1][1] > s:
                at -= 1
            while at < len(taken) and s + dur > taken[at][0]:
                s = max(s, taken[at][1])
                at += 1
            taken.insert(at, (s, s + dur))
        lo_of[k], hi_of[k] = s, s + dur
        for c in after[k]:
            left[c] -= 1
            ready[c] = max(ready[c], s + dur + (0.0 if back else o["lat"]) + WAKE)
            if left[c] == 0:
                cand.append(c)
    return lo_of, hi_of


def order_ops(ops):
    n = len(ops)
    pred = [ops[k]["deps"] | ops[k]["sdeps"] for k in range(n)]
    succ = [[] for _i in range(n)]
    for k in range(n):
        for d in pred[k]:
            succ[d].append(k)
    way = [0.0] * n
    for k in range(n - 1, -1, -1):
        way[k] = ops[k]["dur"] + ops[k]["lat"] + WAKE + max([way[s] for s in succ[k]] or [0.0])
    best = None
    for i in range(PASSES * len(LATES)):
        if i % PASSES == 0:
            key = [(ops[k]["late"] * LATES[i // PASSES] - way[k], k) for k in range(n)]
        lo, hi = place_ops(ops, pred, succ, key, False)
        total = max(hi[k] + ops[k]["lat"] for k in range(n))
        if best is None or total < best[0]:
            best = (total, lo)
        _l, late = place_ops(ops, succ, pred, [(-hi[k] - ops[k]["lat"], -k) for k in range(n)], True)
        key = [(-late[k], k) for k in range(n)]
    order_cache["total"] = best[0]
    return sorted(range(n), key=lambda k: (best[1][k], k))


def emit_ops(g, T, ops, seq):
    known, clk, waits, waited = {}, {}, {}, set()
    pos = {k: i for i, k in enumerate(seq)}
    for k in seq:
        o = ops[k]
        if o["q"] == "recv":
            clk[k] = 0
            continue
        kn = known.get(o["q"], 0)
        w = []
        for d in sorted(o["deps"], key=lambda x: -pos[x]):
            if not (kn >> d) & 1:
                w.append(d)
                waited.add(d)
                kn |= (1 << d) | clk[d]
        known[o["q"]] = kn
        clk[k] = kn
        waits[k] = w
    Q = {"V": g.vector, "P": g.tensor, "S": g.scalar, "Y": g.sync, "G": g}
    last, count, at = {}, {}, {}
    pool = ["p%d" % i for i in range(NPOOL)]
    turn = {}
    for k in seq:
        o = ops[k]
        if o["q"] == "recv":
            at[k] = (o["sem"], o["amount"])
            continue
        q = Q[o["q"]]
        for d in waits[k]:
            q.wait_ge(T.sem[at[d][0]], at[d][1])
        ins = o["emit"]()
        if k in waited:
            if o["sem"] is not None:
                at[k] = (o["sem"], o["amount"])
                ins.then_inc(T.sem[o["sem"]], o["amount"])
            else:
                s = None
                for c in pool:
                    if (c not in last) or (clk[k] >> last[c]) & 1:
                        if s is None or turn.get(c, -1) < turn.get(s, -1):
                            s = c
                            if c not in last:
                                break
                count[s] = count.get(s, 0) + 1
                last[s] = k
                turn[s] = pos[k]
                at[k] = (s, count[s])
                ins.then_inc(T.sem[s], 1)
        elif o["sem"] is not None:
            at[k] = (o["sem"], o["amount"])
            ins.then_inc(T.sem[o["sem"]], o["amount"])
            q.wait_ge(T.sem[o["sem"]], o["amount"])


def rank_program(g, core, T, topo):
    if T.rank_of(core) is None:
        relay_program(g, core, T, topo)
        return
    ops, seq, sent = plan(g, core, T, topo)
    emit_ops(g, T, ops, seq)
    g.wait_ge(T.sem["ls"], sent[0])


def plan(g, core, T, topo):
    rank = T.rank_of(core)
    P = {"late": 0.0, "ops": [], "track": {}, "banks": {"b%d" % i: [] for i in range(8)}}
    C, CP, FAR = 0.00085, CPE, FARUS

    def ap(a):
        if a[0] in POOLED:
            name, at = POOLED[a[0]]
            return T[name][:, at + a[1]:at + a[2]]
        if len(a) > 3:
            return T[a[0]][:, a[1]:a[2]:a[3]]
        return T[a[0]][:, a[1]:a[2]]

    def width(a):
        return len(range(a[1], a[2], a[3] if len(a) > 3 else 1))

    def two(*accs):
        return all((a[0] in SB and SB[a[0]][1] in (F16, BF, U16)) for a in accs)

    def vdur(n, f):
        return 0.01 + C * max(64, n * f)

    def cols(*xs):
        return [x for x in xs if isinstance(x, tuple)]

    def val(x):
        return ap(x) if isinstance(x, tuple) else x

    def copy(out, in_):
        new_op(P, "V", lambda: g.vector.tensor_copy(out=ap(out), in_=ap(in_)), [in_], [out], vdur(width(out), 0.5 if two(out, in_) else 1))

    def ts(out, in0, s1, op0, s2=None, op1=None):
        def e():
            if op1 is None:
                return g.vector.tensor_scalar(out=ap(out), in0=ap(in0), scalar1=val(s1), scalar2=None, op0=op0)
            return g.vector.tensor_scalar(out=ap(out), in0=ap(in0), scalar1=val(s1), scalar2=val(s2), op0=op0, op1=op1)
        new_op(P, "V", e, [in0] + cols(s1, s2), [out], vdur(width(out), 0.5 if two(out, in0) else 1))

    def tt(out, in0, in1, op):
        f = 2 if (in0[0] in SB and in1[0] in SB) else 1
        new_op(P, "V", lambda: g.vector.tensor_tensor(out=ap(out), in0=ap(in0), in1=ap(in1), op=op), [in0, in1], [out], vdur(width(out), f))

    def scan(out, data0, data1, initial, op0, op1):
        new_op(P, "V", lambda: g.vector.tensor_tensor_scan(out=ap(out), data0=ap(data0), data1=ap(data1), initial=val(initial), op0=op0, op1=op1),
               [data0, data1] + cols(initial), [out], vdur(width(out), 1))

    def add_up(out, in_):
        new_op(P, "V", lambda: g.vector.tensor_reduce(out=ap(out), in_=ap(in_), axis=AxisListType.X, op=OP.add), [in_], [out], vdur(width(in_), 1))

    def gather(out, win, off):
        new_op(P, "V", lambda: g.vector.tensor_copy(out=ap(out), in_=ap(win).indirect(ap(off))), [win, off], [out], 0.05 + 1.6 * C * width(out))

    def gather2(out, win, off, in1, op):
        new_op(P, "V", lambda: g.vector.tensor_tensor(out=ap(out), in0=ap(win).indirect(ap(off)), in1=ap(in1), op=op), [win, off, in1], [out],
               0.05 + 1.6 * C * width(out))

    def scatter(win, off, in_):
        new_op(P, "V", lambda: g.vector.tensor_copy(out=ap(win).indirect(ap(off)), in_=ap(in_)), [off, in_], [win], 0.05 + 3.5 * C * width(in_))

    def fill(out, c):
        new_op(P, "V", lambda: g.vector.memset(ap(out), c), [], [out], vdur(width(out), 1))

    def act(out, in_, func, off=None, accum=None, **kw):
        def e():
            src = ap(in_) if off is None else ap(in_).indirect(ap(off))
            more = {k: val(kw[k]) for k in kw}
            if accum is not None:
                more["accum_out"] = ap(accum)
            return g.scalar.activation(out=ap(out), in_=src, func=func, **more)
        dur = 0.02 + C * max(64, width(out)) if off is None else 0.065 + 1.6 * C * width(out)
        new_op(P, "S", e, [in_] + cols(off, *kw.values()), [out] + cols(accum), dur)

    def move(q, out, in_):
        if q == "V":
            copy(out, in_)
        else:
            act(out, in_, AF.Copy)

    def pick(q, out, win, off):
        if q == "V":
            gather(out, win, off)
        else:
            act(out, win, AF.Copy, off=off)

    def mms(*groups):
        def e():
            ins = None
            for out, pairs in groups:
                for i, (l, r) in enumerate(pairs):
                    ins = g.tensor.matmul(ap(out), ap(l), ap(r), i == 0, i == len(pairs) - 1)
            return ins
        dur = 0.02
        for out, pairs in groups:
            dur += len(pairs) * CP * (4 if SB[pairs[0][0][0]][1] == F32 else 1) * max(64, width(out))
        new_op(P, "P", e, [x for o, pairs in groups for p in pairs for x in p], [o for o, pairs in groups], dur)

    def iota(out, pattern, base, cm):
        new_op(P, "G", lambda: g.iota(ap(out), pattern, base, cm), [], [out], 0.13 + 2 * C * width(out))

    loads = []

    def load(q, out, name, sem, lat, also=()):
        eng = g.sync if q == "Y" else g.scalar
        loads.append(new_op(P, q, lambda: eng.dma_start(out=ap(out), in_=T[name][:, :]), [], [out] + list(also), 0.1, sem=sem, amount=16,
                            lat=lat, sdeps=loads[-1:]))

    def store(name, in_, sem):
        new_op(P, "Y", lambda: g.sync.dma_start(out=T[name][:, :], in_=ap(in_)), [in_], [], 0.1, sem=sem, amount=16, lat=2.0)

    sent = [0]
    sends = {}

    def send(sem, after=(), lat=0.0):
        on, src, land, relay = MSG[sem]
        way = route(core, T.cores[(rank + on) % N], topo, relay)

        def e():
            sent[0] += hop(g, T, topo, core, way[1], src, land, sem)
        k = new_op(P, "G", e, [src], [], 0.5, msg=sem, sdeps=[sends[x] for x in after], lat=lat)
        sends[sem] = k
        back = T.cores[(rank - on) % N]
        cnt = len(topo.engines(route(back, core, topo, relay)[-2], core))
        new_op(P, "recv", None, [], [land], 0.0, sem=sem, amount=cnt, sdeps=(k,), lat=FAR)

    def sl(name, at, lo, hi, step=1):
        return (name, at + lo, at + hi) if step == 1 else (name, at + lo, at + hi, step)

    def mat(name, r):
        return (name, 128 * r, 128 * r + 128)

    def full(name):
        return (name, 0, SB[name][0])

    def pieces(sizes):
        return [(sum(sizes[:j]), sum(sizes[:j + 1])) for j in range(len(sizes))]

    def sixteen(name, buf, lo, hi):
        return [(mat(name, r), (buf, lo + r, hi, 16)) for r in range(16)]

    GWIN, XWIN, NB0, IDM = full("GW"), ("XT", 0, 2049), ("NBR", 0, 1152), full("ID")

    load("S", full("TH"), "th", "dm3", 2.5)
    load("S", full("A0"), "a0", "dm2", 0.5)
    loads.clear()
    load("Y", NB0, "nb", "dm0", LOADS[0])
    load("Y", GWIN, "gn", "dm1", LOADS[1])
    load("Y", ("XT", 1, 2049), "x", "dm4", LOADS[2], [("XT", 0, 1)])
    fill(("XT", 0, 1), 0.0)
    iota(full("PI"), [[1, 1]], 0, 1)
    iota(full("MI"), [[1, 128]], 0, 0)
    iota(full("C16"), [[16, 8]], 0, 0)
    iota(full("RI"), [[1, 128]], 128, -1)
    iota(("IOTA", 0, 1152), [[1, 1152]], -1, 0)
    iota(("IOTA", 1152, 2064), [[1, 912]], 1151, 0)
    ts(full("PS"), full("PI"), 4, OP.arith_shift_right)
    ts(full("PL"), full("PI"), 15, OP.bitwise_and)
    copy(full("PSF"), full("PS"))
    copy(full("PLF"), full("PL"))
    ts(full("PL1"), full("PL"), 1.0, OP.add)
    ts(full("PLM"), full("PL"), -1.0, OP.add)
    ts(full("C1S"), full("PL"), 1152.0, OP.mult)
    ts(full("ROWM"), full("PL"), 4.0, OP.is_ge)
    ts(full("ILF"), full("C16"), full("PLF"), OP.add)
    ts(full("L0"), full("ILF"), 9.0, OP.mult)
    ts(full("MS"), full("MI"), 4, OP.arith_shift_right)
    ts(full("ML"), full("MI"), 15, OP.bitwise_and)
    ts(full("ML1"), full("ML"), 1.0, OP.add)
    ts(full("BLK"), full("MS"), full("PSF"), OP.is_equal)
    tt(full("Z"), full("ML1"), full("BLK"), OP.mult)
    ts(IDM, full("Z"), full("PL1"), OP.is_equal)
    ts(full("ZD"), IDM, full("PL1"), OP.mult)
    for r in range(16):
        ts(mat("DIAG", r), full("ZD"), float(r + 1), OP.is_equal)
    for r in range(16):
        ts(mat("CRF", r), full("Z"), float(r + 1), OP.is_equal)
    ts(full("RJ"), full("RI"), 15, OP.bitwise_and)
    ts(full("RK"), full("RJ"), 1.0, OP.add)
    tt(full("ZR"), full("RK"), full("BLK"), OP.mult)
    for r in range(1, 16):
        ts(mat("ROT", r), full("ZR"), float(r + 1), OP.is_equal)
    act(full("NEG3"), mat("CRF", ST - 1), AF.Copy, scale=-1.0)
    fill(full("ZER"), 0.0)
    ts(full("ID2"), IDM, 2.0, OP.mult)
    tt(full("FM"), full("BLK"), full("ID2"), OP.subtract)
    fill(full("QTR"), 0.25)
    scan(full("PW"), full("QTR"), ("ZER", 0, 16), 4.0 ** 16, OP.mult, OP.add)
    ts(full("PW1"), ("MI", 0, 16), full("PLF"), OP.is_equal)
    tt(full("PW1"), full("PW1"), full("PW"), OP.mult)
    add_up(full("WB"), full("PW1"))
    ts(full("FB"), full("FM"), full("WB"), OP.mult)
    act(full("FA"), full("FB"), AF.Copy, scale=4.0 ** 16)
    ts(full("FR"), mat("ROT", 1), -2.0, OP.mult)
    tt(full("FR"), full("FR"), full("BLK"), OP.add)
    ts(full("GB"), full("FR"), full("WB"), OP.mult)
    act(full("GA"), full("GB"), AF.Copy, scale=4.0 ** 16)
    act(full("FH"), full("FR"), AF.Copy, scale=0.25)
    ts(full("M0"), full("ZER"), full("PLF"), OP.is_equal)
    act(full("BLB"), full("BLK"), AF.Copy)
    ts(full("UPR"), full("Z"), full("PL1"), OP.is_ge)
    copy(full("REPL"), ("MI", 0, 64))
    act(full("IDB"), IDM, AF.Copy)
    ts(full("IDR"), IDM, full("ROWM"), OP.mult)
    ts(full("TRI"), full("Z"), full("PL1"), OP.is_gt)
    fill(full("ALL"), 0.0625)
    fill(full("ONES"), 1.0)
    ts(full("KC"), full("ILF"), -1.0, OP.mult, 31.0, OP.add)
    fill(full("BASE"), 0.0)
    fill(full("BASE3"), 0.0)
    for b, (l0, w) in enumerate(BATCH):
        c0, c = l0 // 16, w // 16
        for par in range(3):
            ts(sl("BASE", 32 * par + 4 * c0, c, 2 * c), ("ILF", c0, c0 + c), 16.0, OP.mult, 1.0, OP.add)
        ts(sl("BASE", 4 * c0, 2 * c, 3 * c), ("ILF", c0, c0 + c), 9.0, OP.mult)
        ts(sl("BASE3", 2 * c0, 0, c), ("ILF", c0, c0 + c), 16.0, OP.mult, 1.0, OP.add)
    ts(full("TH1"), full("TH"), 1.0, OP.add)
    ts(("LIM", 0, 1), full("TH"), 1.0, OP.add)
    for j, q in enumerate(NBQ):
        m = 1152 // len(NBQ)
        move(q, ("NBF", m * j, m * j + m), ("NBR", m * j, m * j + m))
    P["late"] = BLATE
    spare = ["b2", "b5", "b6", "b7"]
    for j, lo in enumerate(range(1152, 16 * 1152, 512)):
        hi = min(lo + 512, 16 * 1152)
        bank = spare[j % 4]
        cut = [lo] + [x for x in range(1152, 16 * 1152, 1152) if lo < x < hi] + [hi]
        mms(*[((bank, x - lo, y - lo), [(mat("ROT", x // 1152), ("NBF", x % 1152, x % 1152 + y - x))]) for x, y in zip(cut, cut[1:])])
        move(EVAC[j % len(EVAC)], ("NBR", lo, hi), (bank, 0, hi - lo))
    P["late"] = 0.0

    for gen in range(GENS):
        n0 = gen * ST
        act(("DZ", 128 * n0, 128 * n0 + 128), ("GW", 0, 1152, 9), AF.Copy)
        act(sl("OW", 168 * gen, 0, 128), ("GW", 0, 1152, 9), AF.Copy)
        for h in range(2):
            send("rz%d%d" % (n0, h), lat=6.0 if gen == 0 else 0.0)
        for t in range(ST):
            n = n0 + t
            end = t == ST - 1
            par = 0 if t == 0 else 1 + (n & 1)
            for b, (l0, w) in enumerate(BATCH):
                c0, c = l0 // 16, w // 16
                P["late"] = b
                bA, bB, bC = ["b%d" % (3 * (b % 2) + i) for i in range(3)]
                if n == 0:
                    bC = bA
                o = 2 * (ST - 1 - t)
                tile = lambda name: (name, l0, l0 + w)
                ptile = lambda name: (name, 128 * par + l0, 128 * par + l0 + w)
                wide = lambda name, lo, hi, step=1: sl(name, 16 * l0, lo, hi, step)
                ghm, la, lb = [sl(name, 128 * (n & 1), l0, l0 + w) for name in ("GHM", "LIMA", "LIMB")]
                if t == 0:
                    l1 = l2 = ("L0", c0, c0 + c)
                    nbw, m0 = NB0, tile("M0")
                    a = tile("A0") if gen == 0 else ("LA", 128 * (n - 1) + l0, 128 * (n - 1) + l0 + w)
                else:
                    l1, l2 = lists_at(n, b, o + 3, o + 4), lists_at(n, b, o + 4, o + 5)
                    nbw, m0 = full("NBR"), ("LP", 128 * (n - 1) + l0, 128 * (n - 1) + l0 + w)
                    a = ("LA", 128 * (n - 1) + l0, 128 * (n - 1) + l0 + w)
                nl = lists_at(n, b, o + 4, o + 5)
                base = sl("BASE", 32 * par + 4 * c0, 0, 4 * c)
                if n != ST:
                    gather(ptile("OFF"), nbw, l1)
                    if not end:
                        act(ptile("HT"), ("IOTA", 0, 1152), AF.Identity, off=l2, bias=1.0)
                        gather2(ptile("DH"), nbw, l1, ptile("HT"), OP.subtract)
                if t and not end:
                    copy(sl("BASE", 32 * par + 4 * c0, 2 * c, 3 * c), l2)
                ch = 16 * w // len(GGQ)
                for j, lo in enumerate(range(0, 16 * w, ch)):
                    pick(GGQ[j], wide("GG", lo, lo + ch), GWIN, sl("OFF", 128 * par + l0, lo // 16, (lo + ch) // 16))
                eps = [(lo, (bA if lo == 0 or n == 0 else "b%d" % (6 + b), lo, lo + SUB)) for lo in range(0, w, SUB)]
                for lo, ep in eps:
                    mms((ep, [(IDM, ("ONES", 0, SUB))] + sixteen("DIAG", "GG", 16 * (l0 + lo), 16 * (l0 + lo + SUB))))
                    copy(("EL", l0 + lo, l0 + lo + SUB), ep)
                gather2(ghm, GWIN, l2, m0, OP.mult)
                mms(((bB, 256, 256 + c), [(IDM, ("ONES", 0, c))] + sixteen("CRF", "GHM", ghm[1], ghm[2])))
                copy(nl, (bB, 256, 256 + c))
                gather2(tile("DD"), XWIN, nl, a, OP.subtract)
                for lo, hi in pieces(TCUT):
                    act(wide("TEXP", lo, hi), tile("DD"), AF.Abs, off=("REPL", lo // 16, hi // 16))
                mms(((bC, 192, 192 + w), [(full("UPR"), m0)]))
                ts(la, (bC, 192, 192 + w), ("LIM", n, n + 1), OP.mult)
                ts(lb, (bC, 192, 192 + w), 0.0, OP.is_equal, ("LIM", n, n + 1), OP.mult)
                for lo, hi in pieces(UCUT):
                    gather2(wide("UU", lo, hi), XWIN, sl("EL", l0, lo // 16, hi // 16), wide("TEXP", lo, hi), OP.add)
                for lo, hi in pieces(ACUT):
                    act(wide("AB", lo, hi), wide("UU", lo, hi), AF.Abs, bias=-255.0)
                mms(((bB, 0, w), sixteen("CRF", "AB", 16 * l0, 16 * l0 + 16 * w)))
                tt(tile("OK"), (bB, 0, w), la, OP.is_lt)
                tt(tile("OKB"), (bB, 0, w), lb, OP.is_lt)
                both = [(full("FA"), tile("OK")), (full("FB"), tile("OKB"))]
                fs, fe, tot = (bB, 64, 64 + w), (bB, 128, 128 + w), (bC, 64, 64 + w)
                mms((fs, both), (fe, [(full("FH"), m0), (full("GA"), tile("OK")), (full("GB"), tile("OKB"))]))
                mms((tot, [(full("BLB"), tile("OK")), (full("BLB"), tile("OKB"))]))
                act(tile("NF"), tot, AF.Relu, accum=("RF", b, b + 1), scale=-1.0, bias=1.0)
                pk = lambda j: sl("PACK", 4 * l0, j * w, j * w + w)
                ts(tile("SEL"), fs, 0.0, OP.is_lt)
                sa = ("SA", 128 * n + l0, 128 * n + l0 + w)
                place = sl("POS", 8 * (n & 1), c0, c0 + c)
                if not end:
                    tt(pk(2), tile("SEL"), ptile("DH"), OP.mult)
                    for lo, ep in eps:
                        tt(sl("PACK", 4 * l0 + 3 * w, lo, lo + SUB), sl("SEL", l0, lo, lo + SUB), ep, OP.mult)
                    ts(pk(0), fe, 0.0, OP.is_lt, full("C1S"), OP.mult)
                    ts(pk(1), fe, 0.0, OP.is_lt, full("PLF"), OP.mult)
                    ts(("SP", 128 * n + l0, 128 * n + l0 + w), fe, 0.0, OP.is_lt)
                    send("rp%d%d" % (n, b), after=["rz%d%d" % (n, h) for h in range(2) if t == 0])
                    mms(((bB, 320, 320 + 4 * c), [(IDM, base)] + sixteen("CRF", "PACK", 4 * l0, 4 * l0 + 4 * w)))
                    copy(lists_at(n, b, o + 2, o + 4), (bB, 320 + 2 * c, 320 + 4 * c))
                    new = lists_at(n, b, o + 1, o + 2)
                    for j in range(c):
                        ts(("H", new[1] + j, new[1] + j + 1), (bB, 320 + j, 321 + j), (bB, 320 + 2 * c + j, 321 + 2 * c + j), OP.add)
                    send("rl%d%d" % (n, b), after=["rp%d%d" % (n, b)])
                    copy(place, (bB, 320 + c, 320 + 2 * c))
                    idx, pe = lists_at(n, b, o + 3, o + 4), pk(3)
                else:
                    for lo, ep in eps:
                        tt(sl("PACK", 4 * l0 + w, lo, lo + SUB), sl("SEL", l0, lo, lo + SUB), ep, OP.mult)
                    ts(pk(0), fe, 0.0, OP.is_lt, full("PLF"), OP.mult)
                    mms(((bB, 320, 320 + 2 * c), [(IDM, sl("BASE3", 2 * c0, 0, 2 * c))] + sixteen("CRF", "PACK", 4 * l0, 4 * l0 + 2 * w)))
                    copy(("EN", c0, c0 + c), (bB, 320 + c, 320 + 2 * c))
                    copy(place, (bB, 320, 320 + c))
                    idx, pe = ("EN", c0, c0 + c), pk(1)
                tt(tile("NFT"), tile("NF"), wide("TEXP", 0, 16 * w, 16), OP.mult)
                gather2(sa, XWIN, idx, tile("NFT"), OP.add)
                send("ra%d%d" % (n, b))
                if end:
                    hl = lambda name, lo, hi: sl(name, 6 * c0, lo * c, hi * c)
                    copy(hl("HF", 0, 6), lists_at(n, b, 5, 11))
                    ts(hl("HZ", 0, 6), hl("HF", 0, 6), 0.0, OP.is_equal)
                    tt(hl("HM", 0, 5), hl("HZ", 0, 5), hl("HF", 1, 6), OP.mult)
                    tt(hl("HV", 0, 5), hl("HM", 0, 5), hl("HF", 0, 5), OP.add)
                    copy(hl("VL", 0, 5), hl("HV", 0, 5))
                    tt(("E1", c0, c0 + c), hl("HZ", 0, 1), hl("HZ", 2, 3), OP.add)
                    tt(("E2", c0, c0 + c), ("E1", c0, c0 + c), hl("HZ", 4, 5), OP.add)
                    copy(("EU", c0, c0 + c), ("E2", c0, c0 + c))
                    act(tile("CM"), ("IOTA", 0, 16), AF.Identity, off=("EU", c0, c0 + c), scale=-1.0, bias=full("PLM"))
                    for j in range(ST - 1):
                        act(sl("VT", 128 * j, l0, l0 + w), ("IOTA", 0, 2049), AF.Copy, off=hl("VL", 4 - 2 * j, 5 - 2 * j))
                    tt(tile("IND"), tile("NF"), tile("CM"), OP.is_equal)
                    tt(tile("GHF"), tile("NF"), ghm, OP.mult)
                    mms(((bC, 256, 256 + w), [(full("IDR"), ("DZ", 128 * n + l0, 128 * n + l0 + w))]
                         + [(mat("DIAG", j), sl("VT", 128 * j, l0, l0 + w)) for j in range(ST - 1)]
                         + [(mat("CRF", t), pe), (mat("CRF", t), tile("GHF")), (full("NEG3"), tile("SEL"))]))
                    act(tile("DT"), (bC, 256, 256 + w), AF.Copy)
            P["late"] = 0.0
            if t < ST - 2:
                for h in range(2):
                    send("rz%d%d" % (n + 1, h), after=["ra%d%d" % (n, NBAT - 1)])
            scatter(XWIN, ("POS", 8 * (n & 1), 8 * (n & 1) + 8), ("SA", 128 * n, 128 * n + 128))
            if n < GENS * ST - 1:
                mms(((bC, 128, 129), [(full("ALL"), ("RF", b, b + 1)) for b in range(NBAT)]))
                copy(full("AI"), (bC, 128, 129))
                ts(full("AI2"), full("AI"), 63, OP.bitwise_and)
                ts(("LIM", n + 1, n + 2), full("AI2"), full("TH1"), OP.add)
        add_up(full("NRED"), full("IND"))
        mms((("b7", 0, 1), [(full("TRI"), full("NRED"))]))
        scan(full("PRE"), full("ZER"), full("IND"), ("b7", 0, 1), OP.add, OP.add)
        tt(full("PPK"), full("PRE"), full("IND"), OP.mult)
        q1 = ("b7", 16, 24)
        mms((q1, sixteen("CRF", "PPK", 0, 128)))
        ts(full("POSL"), q1, -1.0, OP.mult, 128.0, OP.add)
        scatter(sl("SD", 136 * gen, 0, 128), full("POSL"), full("DT"))
        ts(full("GEC"), q1, 97.0, OP.is_ge)
        tt(full("DQ"), full("KC"), q1, OP.add)
        tt(full("MLQ"), full("GEC"), full("DQ"), OP.mult)
        tt(sl("SD", 136 * gen, 128, 136), full("MLQ"), full("ILF"), OP.add)
        send("ro%d" % gen)
        send("rm%d" % gen)
        copy(full("IDN"), sl("OW", 168 * gen, 160, 168))
        act(sl("OW", 168 * gen, 128, 160, 2), sl("LO", 32 * gen, 0, 32, 2), AF.Copy)
        gather(("GW", 0, 1152, 9) if gen < GENS - 1 else full("NEW"), sl("OW", 168 * gen, 0, 160), full("IDN"))
    store("yg", full("NEW"), "dm5")
    act(full("YA"), ("LA", 128 * (GENS * ST - 1), 128 * GENS * ST), AF.Copy)
    store("ya", full("YA"), "dm6")
    mms((("b5", 0, 128), [(full("IDB"), ("XT", 1 + j, 2049, 16)) for j in range(16)]))
    act(full("YS"), ("b5", 0, 128), AF.Copy)
    store("ys", full("YS"), "dm7")

    if "seq" not in order_cache:
        order_cache["seq"] = order_ops(P["ops"])
    return P["ops"], order_cache["seq"], sent
